import numpy as np, ml_dtypes
CORES = [40,64,80,88,96,104,120,144]
N = 8
BF = ml_dtypes.bfloat16
def f(rng, *shape):
    return (rng.standard_normal(shape, dtype=np.float32) * np.exp2(rng.integers(-2, 3, shape[:-1] + (1,)))).astype(BF)
def wide(rng, *shape):
    v = f(rng, *shape).astype(np.float32); k = shape[:-2] + (1, shape[-1])
    return (v * np.exp2(rng.integers(-6, 7, k)) * (rng.random(k) > 0.0625)).astype(BF)
def entries(a):
    return np.ascontiguousarray(a.T).reshape(-1)
def table(e):
    return np.ascontiguousarray(np.reshape(e, (-1, 16)).T).astype(np.int32)
def gentries(a):
    return np.ascontiguousarray(a.reshape(8, 16, -1).transpose(0, 2, 1)).reshape(8, -1)
def gtable(e):
    e = np.asarray(e); return np.ascontiguousarray(e.reshape(8, -1, 16).transpose(0, 2, 1)).reshape(128, -1).astype(np.int32)
C, S, STEPS, X, NB = 2048, 32, 5, 1, 128
def others(r):
    a = np.arange(N * S); return a[a // S != r]
def field(v):
    return np.clip(v.astype(np.float32), -16, 16).astype(BF)
def draw(rng, every=False):
    s = rng.integers(0, C, (N, 8, C)); sd = np.zeros((N, N, S), np.int64); inner = []
    for r in range(N):
        p = rng.permutation(C); nb = NB
        if every:
            nb = N * S; p = p[(p > 0) & (p < C - 1)]; e = p[:nb - 2]; p = np.concatenate([[0, C - 1], p])
            sd[r] = np.roll(np.concatenate([[0], e[:2 * S - 2], [C - 1], e[2 * S - 2:]]).reshape(N, S), r + 1, axis=0)
        else:
            sd[r] = np.stack([rng.permutation(p[:nb])[:S] for q in range(N)])
        inner.append(p[nb:])
        s[r][rng.random((8, C)) < 0.125] = -1
        o = others(r)
        for g in range(8): s[r, g, rng.permutation(p[nb:])[:len(o)]] = C + rng.permutation(o)
    return s, sd, inner
def pack(rng, s, sd):
    m = [(rng.standard_normal((128, 128)) * 128 ** -0.5 * z).clip(-1, 1).astype(BF) for z in (0.85, 1.0)]
    return {"flow": field(f(rng, N, 128, C).astype(np.float32) * np.float32(0.5)), "mix": np.stack([m[0]] * N), "bend": np.stack([m[1]] * N),
            "links": np.stack([gtable(s[r]) for r in range(N)]), "sends": np.stack([table(sd[r].reshape(-1)) for r in range(N)])}
def setup_inputs(rng):
    s, sd, inner = draw(rng); return pack(rng, s, sd)
def setup_inputs_walls(rng):
    s, sd, inner = draw(rng, True)
    for r in range(N):
        o = rng.permutation(8); s[r][:, rng.permutation(C)[:256]] = -1; s[r][:, [0, C - 1]] = -1
        s[r, o[0]] = -1; s[r, o[1]] = np.where(s[r, o[1]] < 0, np.arange(C), s[r, o[1]])
    return pack(rng, s, sd)
def setup_inputs_repeats(rng):
    s, sd, inner = draw(rng)
    for r in range(N):
        o = rng.permutation(8); c = rng.integers(0, C, 8); c[o[0]] = 0; c[o[1]] = C - 1; e = others(r)
        near = (s[r] >= 0) & (s[r] < C) & (rng.random((8, C)) < 0.75)
        s[r] = np.where(near, c[:, None], s[r])
        s[r, o[2]] = np.where(s[r, o[2]] >= C, C + e[-1], s[r, o[2]]); s[r, o[3]] = np.where(s[r, o[3]] >= C, C + e[0], s[r, o[3]])
        sd[r, (r + 1) % N] = sd[r, (r + 1) % N, 0]
    return pack(rng, s, sd)
def setup_inputs_far(rng):
    s, sd, inner = draw(rng)
    for r in range(N):
        e = others(r); k = inner[r]; s[r][:, k] = C + rng.choice(e, (8, len(k)))
        s[r][:, k[0]] = C + e[0]; s[r][:, k[1]] = C + e[-1]
    return pack(rng, s, sd)
def setup_inputs_spread(rng):
    d = setup_inputs(rng); d["flow"] = field(wide(rng, N, 128, C).astype(np.float32) * np.float32(2.0 ** -7)); return d
def check_inputs(d):
    bad = []
    for a, b in (("flow", 16), ("mix", 1), ("bend", 1)):
        x = d[a].astype(np.float64)
        if not (np.abs(x) <= b).all(): bad.append(a + ": size")
        if a != "flow" and not (x == x[:1]).all(): bad.append(a + ": not alike on all ranks")
    s = np.stack([gentries(d["links"][r]) for r in range(N)]).astype(np.int64); sd = np.stack([entries(d["sends"][r]) for r in range(N)]).astype(np.int64)
    if (s < -1).any() or (s >= C + N * S).any(): bad.append("links: range")
    if (sd < 0).any() or (sd >= C).any(): bad.append("sends: range")
    if bad: return bad
    for r in range(N):
        if ((s[r] >= C) & ((s[r] - C) // S == r)).any(): bad.append("links: own rank's arrivals")
        if (s[r][:, sd[r]] >= C).any(): bad.append("a cell that is sent takes from another rank")
    if not bad:
        with np.errstate(all="ignore"): v, top = run(**d)
        if not (top <= 1024): bad.append("h or v of a step: size")
    return bad
def run(flow, mix, bend, links, sends):
    v = flow.astype(np.float64); m = mix.astype(np.float64); b = bend.astype(np.float64); top = 0.0
    s = np.stack([gentries(links[r]) for r in range(N)]).astype(np.int64)[:, :, None, :]
    sd = np.stack([entries(sends[r]).reshape(N, S) for r in range(N)]).astype(np.int64)
    opp = np.arange(8) ^ X
    for t in range(STEPS):
        h = np.stack([m[r].T @ v[r] + 0.125 * (b[r].T @ v[r]) ** 2 for r in range(N)])
        top = np.maximum(top, np.max(np.abs(h)))
        new = []
        for r in range(N):
            w = np.concatenate([h[r]] + [h[q][:, sd[q, r]] for q in range(N)], axis=1).reshape(8, 16, C + N * S)
            got = np.take_along_axis(w, np.maximum(s[r], 0), axis=2)
            new.append(np.where(s[r] < 0, h[r].reshape(8, 16, C)[opp], got).reshape(128, C))
        v = np.stack(new)
    return v, top
def reference(flow, mix, bend, links, sends):
    v, top = run(flow, mix, bend, links, sends)
    return {"y": v.astype(np.float32)}

@@ -1,0 +1,481 @@
+import math
+from concourse.bass import DstId, RemoteDMATransfer
+from concourse.mybir import AluOpType as ALU, ActivationFunctionType as ACT
+
+C, S, N, STEPS = 2048, 32, 8, 5
+NS = (N - 1) * S
+H0 = NS
+A0 = H0 + C
+W0 = A0 + N * S
+WIDTH = W0 + C
+ORDER = [0, 3, 4, 7, 1, 2, 5, 6]
+RUNS = [(0, 1), (1, 3), (3, 4), (4, 6), (6, 8)]
+FIRST = [512, 512, 512, 384, 128]
+MAIN = [(256, "f?"), (512, "f?"), (256, "saa"), (256, "saa"), (256, "saa"), (320, "f?"), (128, "f?"), (64, "f?")]
+SECOND = [(128, "f?"), (128, "f?")] + MAIN[1:]
+GIVEN = [64, 64, 96]
+LAST = [256, 512, 640, 640]
+BY_ENGINE = [9, 0, 0, 0, 2]
+MERGE = 256
+ALL16 = False
+ROUNDS = 6
+LAT = [9000, 3500]
+PLANS = [(1.0, 1.56, 0.5, 100.0), (0.9, 1.2, 0.45, 80.0), (1.15, 1.95, 0.55, 130.0)]
+
+SCRATCH = {"wr": ("sbuf", [128, 2, 128], "bfloat16"), "wc": ("sbuf", [128, 2, 128], "bfloat16")}
+for _d, _l in (("bfloat16", [("fl", C), ("wb", 256), ("ones", 64), ("pm", 128), ("vs0", NS), ("hi", C), ("md", C), ("lo", C)]),
+               ("float32", [("wf", 256), ("bo", 128), ("i8", 128), ("i16", NS), ("dg", NS), ("nd", NS), ("ic", 128),
+                            ("nk", 128), ("mj", 16), ("pf", 4), ("sf", 16), ("gt", 128), ("go", 128), ("m1", NS),
+                            ("qm", NS), ("rd", NS), ("sc", NS), ("t1", 16), ("t2", 16), ("vf", NS + C), ("sq", NS + C),
+                            ("rr", C), ("sb", STEPS * NS)] + [("w%d" % _t, WIDTH) for _t in range(STEPS)]),
+               ("int32", [("pc", 4), ("pd", 4), ("s16", 16), ("si", 16), ("sh", 32), ("gi", 128)]),
+               ("uint16", [("su", 16), ("shu", 32), ("off", 128), ("offs", 16)])):
+    for _n, _w in _l:
+        SCRATCH[_n] = ("sbuf", [128, _w], _d)
+for _b in range(8):
+    SCRATCH["ps%d" % _b] = ("psum", [128, 512], "float32")
+
+SEMAPHORES = (["q_pe", "q_act", "q_dve", "q_pool", "sent", "d_s", "d_f", "d_w", "d_b", "d_l", "d_y"]
+              + ["arr%d" % t for t in range(STEPS)] + ["rly%d" % t for t in range(STEPS)]
+              + ["sw%d_%d" % (t, k) for t in range(STEPS) for k in range(12)])
+
+
+def routes(T, topo, r):
+    me = T.cores[r]
+    far = [q for q in range(N) if q != r and not topo.may_write(me, T.cores[q])]
+    near = [q for q in range(N) if q != r and q not in far]
+    able = [c for c in topo.cores_of(me)
+            if c != me and T.rank_of(c) is None and all(topo.may_write(c, T.cores[q]) for q in far)]
+    able.sort(key=lambda c: topo.die(c) != topo.die(me))
+    half = (len(far) + 1) // 2
+    return far, near, [(able[0], far[:half]), (able[1], far[half:])]
+
+
+def deal(engines, k):
+    sizes = [len(engines)]
+    while len(sizes) < k:
+        sizes.sort()
+        big = sizes.pop()
+        sizes += [big // 2, big // 2]
+    sizes.sort(reverse=True)
+    out, at = [], 0
+    for s in sizes:
+        out.append((sum(1 << e for e in engines[at:at + s]), s))
+        at += s
+    return out
+
+
+def arrivals(T, topo, r):
+    n = 0
+    for q in range(N):
+        if q != r:
+            far, near, relays = routes(T, topo, q)
+            for c, ds in relays + [(T.cores[q], near)]:
+                if r in ds:
+                    n += deal(topo.engines(c, T.cores[r]), len(ds))[ds.index(r)][1]
+    return n
+
+
+def inward(T, topo, r):
+    me = T.cores[r]
+    far, near, relays = routes(T, topo, r)
+    out = topo.engines(me, T.cores[near[0]])
+    return deal([e for e in topo.engines(me, relays[0][0]) if ALL16 or e not in out], len(relays))
+
+
+def outward(T, topo, core, r, ds, t, at):
+    tr, n = [], 0
+    for i, (q, (m, k)) in enumerate(zip(ds, deal(topo.engines(core, T.cores[ds[0]]), len(ds)))):
+        rid, pid = topo.addr(T.cores[q], core)
+        tr.append(RemoteDMATransfer(dst_ids=[DstId(rid=rid, pnc=pid)], dma_engine_mask=m,
+                                    remote_sem=T.sem["arr%d" % t], src=T.sb[:, at + i * S:at + (i + 1) * S],
+                                    dst=T["w%d" % t][:, A0 + r * S:A0 + (r + 1) * S]))
+        n += k
+    return tr, n
+
+
+def relay_program(g, core, T, topo, r, k):
+    total = 0
+    for t in range(STEPS):
+        g.wait_ge(T.sem["rly%d" % t], inward(T, topo, r)[k][1])
+        tr, n = outward(T, topo, core, r, routes(T, topo, r)[2][k][1], t, t * NS)
+        g.remote_dma_fused(tr, local_sem=T.sem.sent)
+        total += n
+    g.wait_ge(T.sem.sent, total)
+
+
+def build_ops(g, core, T, topo, r):
+    ops = []
+    V, A, P = g.vector, g.scalar, g.tensor
+
+    def op(alts, rd, wr, sem=None, lat=0.0, after=(), behind=()):
+        ops.append({"alts": alts, "rd": rd, "wr": wr, "sem": sem, "lat": lat, "after": list(after),
+                    "behind": list(behind)})
+        return len(ops) - 1
+
+    def R(buf, a=0, b=1 << 20, p=0, q=128):
+        return (buf, a, b, p, q)
+
+    def ve(n, f, rd, wr, c=1, behind=()):
+        return op([("dve", (40, max(64, n * c), 0, 0), f)], rd, wr, behind=behind)
+
+    def vg(n, f, rd, wr):
+        return op([("dve", (50, 0, n, 0), f)], rd, wr)
+
+    def copy(n, out, in_, rd, wr, gather=False, only=None, behind=()):
+        cv = (50, 0, n, 0) if gather else (40, max(64, n), 0, 0)
+        ca = (65, 0, n, 0) if gather else cv
+        alts = [("dve", cv, lambda: V.tensor_copy(out, in_)), ("act", ca, lambda: A.activation(out, in_, ACT.Copy))]
+        return op([x for x in alts if only in (None, x[0])], rd, wr, behind=behind)
+
+    def mm(n, out, lhsT, rhs, start, stop, rd, bank, wide, after=()):
+        return op([("pe", (10, 0, 0, max(64, n) * (4 if wide else 1)), lambda: P.matmul(out, lhsT, rhs, start, stop))],
+                  rd, [R(bank)], after=after)
+
+    def pool(ns, f, rd, wr):
+        return op([("pool", (ns, 0, 0, 0), f)], rd, wr)
+
+    def dma(q, pairs, sem, rd, wr, rows, size, behind=()):
+        e = g.sync if q == "sp" else g.scalar
+        x = op([(q, (60 * len(pairs), 0, 0, 0), lambda: [e.dma_start(o, i) for o, i in pairs])], rd, wr,
+               sem=(sem, 16 * len(pairs)), lat=800, behind=behind)
+        op([("dq", (rows * (40 + size / 25) / 16, 0, 0, 0), None)], [], wr, sem=x, lat=900, after=[x],
+           behind=[j + 1 for j in behind])
+        return x
+
+    far, near, relays = routes(T, topo, r)
+    nfar = len(far) * S
+    K = NS // 16
+
+    x = dma("sp", [(T.s16[0:16, :], T.sends[:])], "d_s", [], [R("s16")], 16, 64)
+    m = dma("act", [(T.wr[:, 0, :], T.mix[:])], "d_w", [], [R("wr", 0, 1)], 128, 256)
+    x = dma("sp", [(T.wr[:, 1, :], T.bend[:])], "d_b", [], [R("wr", 1, 2)], 128, 256, [x])
+    x = dma("sp", [(T.fl[:], T.flow[:])], "d_f", [], [R("fl")], 128, 4096, [x, m])
+    dma("sp", [(T.gi[16 * a:16 * b, :], T.links[16 * ORDER[a]:16 * (ORDER[a] + b - a), :]) for a, b in RUNS],
+        "d_l", [], [R("gi")], 128, 512, [x])
+
+    imp = {"allow_small_or_imprecise_dtypes": True}
+    pool(140, lambda: g.iota(T.pc[:, 0:1], [[0, 1]], 0, 1), [], [R("pc")])
+    pool(560, lambda: g.iota(T.i16[:], [[0, K], [1, 16]], 0, 0, **imp), [], [R("i16")])
+    ve(1, lambda: V.tensor_scalar(T.pd[:, 0:1], T.pc[:, 0:1], 15, None, ALU.bitwise_and), [R("pc")], [R("pd", 0, 1)])
+    ve(1, lambda: V.tensor_scalar(T.pd[:, 1:2], T.pc[:, 0:1], 4, None, ALU.arith_shift_right), [R("pc")], [R("pd", 1, 2)])
+    ve(2, lambda: V.tensor_copy(T.pf[:, 0:2], T.pd[:, 0:2]), [R("pd")], [R("pf")])
+    ve(NS, lambda: V.tensor_scalar(T.dg[:], T.i16[:], T.pf[:, 0:1], None, ALU.is_equal), [R("i16"), R("pf")], [R("dg")])
+    ve(64, lambda: V.memset(T.ones[:], 1.0), [], [R("ones")])
+    for t in range(STEPS):
+        ve(S, lambda t=t: V.memset(T["w%d" % t][:, A0 + r * S:A0 + (r + 1) * S], 0.0), [],
+           [R("w%d" % t, A0 + r * S, A0 + (r + 1) * S)])
+    for a in range(2):
+        o = ORDER[4 * a:4 * a + 4]
+        pat = [[-16 * (o[2] - o[0]), 2], [-16 * (o[1] - o[0]), 2], [-1, 16]]
+        pool(300, lambda a=a, o=o, pat=pat: g.affine_select(T.pm[:, 64 * a:64 * a + 64], T.ones[:], pat, ALU.is_equal,
+                                                            0.0, -16 * o[0], 1), [R("ones")], [R("pm", 64 * a, 64 * a + 64)])
+    pool(380, lambda: g.iota(T.i8[:], [[1, 8], [0, 16]], 0, 0, **imp), [], [R("i8")])
+    pool(380, lambda: g.iota(T.ic[:], [[-16, 128]], -(W0 - H0), 0, **imp), [], [R("ic")])
+
+    runs = []
+    for i, q in enumerate(far + near):
+        if runs and runs[-1][1] + runs[-1][2] == q:
+            runs[-1][2] += 1
+        else:
+            runs.append([i, q, 1])
+    for i, q, n in runs:
+        ve(2 * n, lambda i=i, q=q, n=n: V.tensor_copy(T.sf[0:16, 2 * i:2 * (i + n)], T.s16[0:16, 2 * q:2 * (q + n)]),
+           [R("s16")], [R("sf", 2 * i, 2 * (i + n))])
+    mm(K, T.ps6[:, 0:K], T.dg[0:16, 0:128], T.sf[0:16, 0:K], True, True, [R("dg"), R("sf")], "ps6", True)
+    ve(K, lambda: V.tensor_copy(T.su[:, 0:K], T.ps6[:, 0:K]), [R("ps6")], [R("su")])
+    ve(K, lambda: V.tensor_copy(T.si[:, 0:K], T.ps6[:, 0:K]), [R("ps6")], [R("si")])
+
+    for a, b in RUNS:
+        x = 16 * ORDER[a]
+        op([("act", (40, 64, 0, 0), lambda a=a, b=b, x=x: A.activation(
+            T.wc[:, :, 16 * a:16 * b], T.wr[:, :, x:x + 16 * (b - a)], ACT.Copy))], [R("wr")], [R("wc", 16 * a, 16 * b)])
+
+    def late_setup(x):
+        m0 = mm(128, T.ps7[:, 0:128], T.pm[:], T.wc[:, 0, :], True, True, [R("pm"), R("wc")], "ps7", False)
+        mm(128, T.ps7[:, 128:256], T.pm[:], T.wc[:, 1, :], True, True, [R("pm"), R("wc")], "ps7", False, after=[m0])
+        copy(256, T.wf[:], T.ps7[:, 0:256], [R("ps7")], [R("wf")])
+        copy(256, T.wb[:], T.wf[:], [R("wf")], [R("wb")])
+        ve(NS, lambda: V.tensor_scalar(T.nd[:], T.i16[:], T.pf[:, 0:1], None, ALU.not_equal), [R("i16"), R("pf")], [R("nd")], behind=x)
+        ve(128, lambda: V.tensor_scalar(T.bo[:], T.i8[:], T.pf[:, 1:2], None, ALU.is_equal), [R("i8"), R("pf")], [R("bo")], behind=x)
+        ve(128, lambda: V.tensor_scalar(T.nk[:], T.ic[:], T.pf[:, 0:1], None, ALU.subtract), [R("ic"), R("pf")], [R("nk")], behind=x)
+        ve(16, lambda: V.tensor_scalar(T.mj[:], T.nk[:, 0:16], float(W0 - H0 + NS), None, ALU.add), [R("nk")], [R("mj")])
+        ve(128, lambda: V.tensor_tensor(T.gt[:], T.gi[:], T.nk[:], ALU.mult), [R("gi"), R("nk")], [R("gt")], 2)
+        ve(128, lambda: V.tensor_tensor(T.go[:], T.gi[:], T.gt[:], ALU.max), [R("gi"), R("gt")], [R("go")], 2)
+        ve(128, lambda: V.tensor_copy(T.off[:], T.go[:]), [R("go")], [R("off")])
+        ve(K, lambda: V.tensor_scalar(T.sh[:, 0:K], T.si[:, 0:K], 4, None, ALU.arith_shift_right), [R("si")], [R("sh", 0, K)], behind=x)
+        ve(K, lambda: V.tensor_scalar(T.sh[:, K:2 * K], T.si[:, 0:K], 15, None, ALU.bitwise_and), [R("si")], [R("sh", K, 2 * K)], behind=x)
+        ve(2 * K, lambda: V.tensor_copy(T.shu[:, 0:2 * K], T.sh[:, 0:2 * K]), [R("sh")], [R("shu")])
+        copy(NS, T.m1[:], T.dg[:, 0:16].indirect(T.shu[:, K:2 * K]), [R("dg"), R("shu")], [R("m1")], gather=True)
+        vg(NS, lambda: V.tensor_tensor(T.qm[:], T.gi[:, 0:128].indirect(T.shu[:, 0:K]), T.m1[:], ALU.mult),
+           [R("gi"), R("shu"), R("m1")], [R("qm")])
+        mm(NS, T.ps7[:, 0:NS], T.bo[:], T.qm[:], True, True, [R("bo"), R("qm")], "ps7", True)
+        ve(NS, lambda: V.tensor_tensor(T.rd[:], T.ps7[:, 0:NS], T.dg[:], ALU.mult), [R("ps7"), R("dg")], [R("rd")])
+        ve(NS, lambda: V.tensor_tensor_scan(T.sc[:], T.nd[:], T.rd[:], 0.0, ALU.mult, ALU.add), [R("nd"), R("rd")], [R("sc")])
+        ve(K, lambda: V.tensor_tensor(T.t1[:, 0:K], T.sc[:, 15:NS:16], T.mj[:, 0:K], ALU.mult), [R("sc"), R("mj")], [R("t1")])
+        ve(K, lambda: V.tensor_tensor(T.t2[:, 0:K], T.sc[:, 15:NS:16], T.t1[:, 0:K], ALU.min), [R("sc"), R("t1")], [R("t2")])
+        ve(K, lambda: V.tensor_scalar(T.offs[:, 0:K], T.t2[:, 0:K], float(NS), None, ALU.add), [R("t2")], [R("offs")])
+
+    chain = []
+    who = {"a": "act", "v": "dve", "?": None}
+    root = math.sqrt(0.125)
+
+    def collide(n, pieces, wbuf, x, out, outr):
+        k = len(chain) % 4
+        ba, bb = "ps%d" % (2 * k), "ps%d" % (2 * k + 1)
+        pa, pb = T[ba][:, 0:n], T[bb][:, 0:n]
+        wm, wbd = (T.wc[:, 0, :], T.wc[:, 1, :]) if wbuf == "wc" else (T[wbuf][:, 0:128], T[wbuf][:, 128:256])
+        last = chain[-1:]
+        for i, (ap, reg) in enumerate(pieces):
+            st, sp = i == 0, i == len(pieces) - 1
+            last = [mm(n, pb, wbd, ap, st, sp, [R(wbuf), reg], bb, wbuf == "wf", after=last)]
+            last = [mm(n, pa, wm, ap, st, sp, [R(wbuf), reg], ba, wbuf == "wf", after=last)]
+        chain.append(last[0])
+        op([("act", (40, max(64, n), 0, 0), lambda: A.activation(T.sq[:, x:x + n], pb, ACT.Square, scale=root))],
+           [R(bb)], [R("sq", x, x + n)])
+        return ve(n, lambda: V.tensor_tensor(out, pa, T.sq[:, x:x + n], ALU.add), [R(ba), R("sq", x, x + n)], [outr])
+
+    def swap(sname, a, n, wn, b, sem, engine):
+        src = T[sname]
+        if engine:
+            for p in (0, 64):
+                copy(n, T[wn][64 - p:128 - p, b:b + n], src[p:p + 64, a:a + n], [R(sname, a, a + n)],
+                     [R(wn, b, b + n, 64 - p, 128 - p)])
+        else:
+            dma("sp", [(T[wn][64:128, b:b + n], src[0:64, a:a + n]), (T[wn][0:64, b:b + n], src[64:128, a:a + n])],
+                sem, [R(sname, a, a + n)], [R(wn, b, b + n)], 128, 4 * n)
+
+    def call(t, part):
+        if part == 0:
+            tr, n, at = [], 0, t * NS
+            for (c, ds), (m, k) in zip(relays, inward(T, topo, r)):
+                rid, pid = topo.addr(c, core)
+                wd = len(ds) * S
+                tr.append(RemoteDMATransfer(dst_ids=[DstId(rid=rid, pnc=pid)], dma_engine_mask=m,
+                                            remote_sem=T.sem["rly%d" % t], src=T.sb[:, at:at + wd],
+                                            dst=T.sb[:, t * NS:t * NS + wd]))
+                at += wd
+                n += k
+        else:
+            tr, n = outward(T, topo, core, r, near, t, t * NS + nfar)
+        a, b = (0, nfar) if part == 0 else (nfar, NS)
+        return op([("pool", (3000 if t + part == 0 else 900, 0, 0, 0), lambda: g.remote_dma_fused(tr, local_sem=T.sem.sent))],
+                  [R("sb", t * NS + a, t * NS + b)], [], sem=("sent", n), lat=3000)
+
+    narr = arrivals(T, topo, r)
+    for t in range(STEPS):
+        wn, wp = "w%d" % t, "w%d" % (t - 1)
+        calls, b = [], 0
+        for n in GIVEN:
+            a, b = b, b + n
+            x = t * NS + a
+            if t == 0:
+                copy(n, T.vs0[:, a:b], T.fl[:, 0:C].indirect(T.su[:, a // 16:b // 16]), [R("fl"), R("su")],
+                     [R("vs0", a, b)], gather=True)
+                done = collide(n, [(T.vs0[:, a:b], R("vs0", a, b))], "wc", a, T.sb[:, x:x + n], R("sb", x, x + n))
+            else:
+                copy(n, T.vf[:, a:b], T[wp][:, 0:A0].indirect(T.offs[:, a // 16:b // 16]),
+                     [R(wp, 0, A0), R("offs")], [R("vf", a, b)], gather=True)
+                collide(n, [(T.vf[:, a:b], R("vf", a, b))], "wf", a, T.sb[:, x:x + n], R("sb", x, x + n))
+            calls += [call(t, part) for part, e in enumerate((nfar, NS)) if e == b]
+        if t < STEPS - 1:
+            swap("sb", t * NS, NS, wn, 0, "sw%d_11" % t, BY_ENGINE[t] > 8)
+        blocks = [R(wn, A0 + q * S, A0 + (q + 1) * S) for q in range(N) if q != r]
+        op([(None, (0, 0, 0, 0), None)], [], blocks, sem=("arr%d" % t, narr), lat=LAT[min(t, 1)], after=calls)
+        c0 = s0 = 0
+        chunks = [(n, "b") for n in FIRST] if t == 0 else SECOND if t == 1 else MAIN
+        for k, (n, mode) in enumerate(chunks):
+            c1, x = c0 + n, NS + c0
+            out, outr = T[wn][:, H0 + c0:H0 + c1], R(wn, H0 + c0, H0 + c1)
+            if mode != "b":
+                src = T[wp][:, H0:W0 + c1].indirect(T.off[:, c0 // 16:c1 // 16])
+                rd = [R(wp, H0, W0 + c1), R("off")]
+            if mode == "b":
+                collide(n, [(T.fl[:, c0:c1], R("fl"))], "wc", x, out, outr)
+            elif mode[0] == "f":
+                copy(n, T.vf[:, x:x + n], src, rd, [R("vf", x, x + n)], gather=True, only=who[mode[1]])
+                collide(n, [(T.vf[:, x:x + n], R("vf", x, x + n))], "wf", x, out, outr)
+            else:
+                hi, md, lo, rr = T.hi[:, c0:c1], T.md[:, c0:c1], T.lo[:, c0:c1], T.rr[:, c0:c1]
+                copy(n, hi, src, rd, [R("hi", c0, c1)], gather=True, only=who[mode[1]])
+                vg(n, lambda rr=rr, src=src, hi=hi: V.tensor_tensor(rr, src, hi, ALU.subtract),
+                   rd + [R("hi", c0, c1)], [R("rr", c0, c1)])
+                copy(n, md, rr, [R("rr", c0, c1)], [R("md", c0, c1)], only=who[mode[2]])
+                ve(n, lambda lo=lo, rr=rr, md=md: V.tensor_tensor(lo, rr, md, ALU.subtract),
+                   [R("rr", c0, c1), R("md", c0, c1)], [R("lo", c0, c1)], 2)
+                collide(n, [(hi, R("hi", c0, c1)), (md, R("md", c0, c1)), (lo, R("lo", c0, c1))], "wb", x, out, outr)
+            left = len(chunks) - k
+            if c1 - s0 >= MERGE or left <= BY_ENGINE[t] + 1:
+                swap(wn, H0 + s0, c1 - s0, wn, W0 + s0, "sw%d_%d" % (t, k), left <= BY_ENGINE[t])
+                s0 = c1
+            c0 = c1
+            if t == 0 and k == 1:
+                late_setup([done])
+
+    wp = "w%d" % (STEPS - 1)
+    c0, x = 0, []
+    for n in LAST:
+        c1, h = c0 + n, n // 2
+        for a in (c0, c0 + h):
+            copy(h, T.vf[:, NS + a:NS + a + h], T[wp][:, H0:W0 + a + h].indirect(T.off[:, a // 16:(a + h) // 16]),
+                 [R(wp, H0, W0 + a + h), R("off")], [R("vf", NS + a, NS + a + h)], gather=True)
+        x = [dma("sp", [(T.y[16 * ORDER[a]:16 * (ORDER[a] + b - a), c0:c1], T.vf[16 * a:16 * b, NS + c0:NS + c1])
+                        for a, b in RUNS], "d_y", [R("vf", NS + c0, NS + c1)], [], 128, 4 * n, x)]
+        c0 = c1
+    return ops
+
+
+def order_ops(ops):
+    seen = {}
+    for i, o in enumerate(ops):
+        dep = set(o["after"])
+        acc = [(x, x[0].startswith("ps")) for x in o["rd"]] + [(x, True) for x in o["wr"]]
+        for x, w in acc:
+            for j, y, v in seen.get(x[0], []):
+                if (w or v) and x[1] < y[2] and y[1] < x[2] and x[3] < y[4] and y[3] < x[4]:
+                    dep.add(j)
+        for x, w in acc:
+            lst = seen.setdefault(x[0], [])
+            if w:
+                lst[:] = [e for e in lst if not (x[1] <= e[1][1] and e[1][2] <= x[2] and x[3] <= e[1][3] and e[1][4] <= x[4])]
+            lst.append((i, x, w))
+        o["dep"] = sorted(dep)
+    n = len(ops)
+    pre = [[(j, 1) for j in o["dep"]] + [(j, 0) for j in o["behind"]] for o in ops]
+    post = [[] for o in ops]
+    for i in range(n):
+        for j, w in pre[i]:
+            post[j].append((i, w))
+
+    def ns(c, p):
+        return c[0] + (c[1] + c[2] * p[1]) * p[0] + c[3] * p[2]
+
+    def place(busy, q, t, cost):
+        for s, e in busy.get(q, []):
+            if t + cost <= s:
+                break
+            t = max(t, e)
+        return t
+
+    def take(busy, q, t, cost):
+        if q is not None:
+            busy.setdefault(q, []).append((t, t + cost))
+            busy[q].sort()
+
+    def forward(seq, p, bias):
+        busy, st, en, pick = {}, [0.0] * n, [0.0] * n, [0] * n
+        for i in seq:
+            best = None
+            for a, (q, c, emit) in enumerate(ops[i]["alts"]):
+                cost, t = ns(c, p), 0.0
+                for j, w in pre[i]:
+                    qj = ops[j]["alts"][pick[j]][0]
+                    t = max(t, en[j] + (0.0 if q == qj == "pe" else p[3]) if w else en[j] - ops[j]["lat"])
+                t = place(busy, q, t, cost)
+                key = t + cost + (bias if q == "dve" else 0.0)
+                if best is None or key < best[0]:
+                    best = (key, a, t, cost, q)
+            pick[i], st[i], en[i] = best[1], best[2], best[2] + best[3] + ops[i]["lat"]
+            take(busy, best[4], best[2], best[3])
+        return st, en, pick
+
+    def backward(en, pick, p):
+        busy, fin = {}, [0.0] * n
+        for i in sorted(range(n), key=lambda i: (-en[i], -i)):
+            q, c, emit = ops[i]["alts"][pick[i]]
+            cost, t = ns(c, p), ops[i]["lat"]
+            for j, w in post[i]:
+                qj = ops[j]["alts"][pick[j]][0]
+                t = max(t, fin[j] + ops[i]["lat"] + (0.0 if q == qj == "pe" else p[3]) if w else fin[j])
+            t = place(busy, q, t, cost)
+            fin[i] = t + cost
+            take(busy, q, t, cost)
+        return fin
+
+    def replay(seq, pick, p):
+        free, en = {}, [0.0] * n
+        for i in seq:
+            q, c, emit = ops[i]["alts"][pick[i]]
+            t = free.get(q, 0.0)
+            for j, w in pre[i]:
+                if w:
+                    t = max(t, en[j] + (0.0 if q == ops[j]["alts"][pick[j]][0] == "pe" else p[3]))
+            if q is not None:
+                free[q] = t + ns(c, p)
+            en[i] = t + ns(c, p) + ops[i]["lat"]
+        return max(en)
+
+    def legal(key):
+        for i in range(n - 1, -1, -1):
+            for j, w in pre[i]:
+                key[j] = max(key[j], key[i])
+        return sorted(range(n), key=lambda i: (-key[i], i))
+
+    best, seed, p = None, 12345, PLANS[0]
+    for bias in (0.0, 150.0, 400.0):
+        key = [0.0] * n
+        for i in range(n - 1, -1, -1):
+            key[i] += min(ns(a[1], p) for a in ops[i]["alts"]) + ops[i]["lat"] + p[3]
+            for j, w in pre[i]:
+                key[j] = max(key[j], key[i])
+        for rnd in range(ROUNDS):
+            st, en, pick = forward(legal(key), p, bias)
+            seq = sorted(range(n), key=lambda i: (st[i], i))
+            score = sum(replay(seq, pick, x) for x in PLANS)
+            if best is None or score < best[0]:
+                best = (score, seq, en, pick)
+            key = backward(en, pick, p)
+            for i in range(n):
+                seed = (seed * 1103515245 + 12345) % 2147483648
+                key[i] += 200.0 * (rnd % 3) * seed / 2147483648
+    score, seq, en, pick = best
+    for i, o in enumerate(ops):
+        o["q"], o["emit"], o["end"] = o["alts"][pick[i]][0], o["alts"][pick[i]][2], en[i]
+    return seq
+
+
+def rank_program(g, core, T, topo):
+    r = T.rank_of(core)
+    if r is None:
+        for q in range(N):
+            for k, (c, ds) in enumerate(routes(T, topo, q)[2]):
+                if c == core:
+                    relay_program(g, core, T, topo, q, k)
+        return
+    ops = build_ops(g, core, T, topo, r)
+    eng = {"pe": g.tensor, "act": g.scalar, "dve": g.vector, "pool": g, "sp": g.sync}
+    known = {q: {} for q in eng}
+    total = {}
+    for i in order_ops(ops):
+        o = ops[i]
+        q = o["q"]
+        if q is None:
+            o["mark"], o["clock"] = o["sem"], {o["sem"][0]: o["sem"][1]}
+            total[o["sem"][0]] = o["sem"][1]
+            continue
+        if q == "dq":
+            o["mark"], o["clock"] = ops[o["sem"]]["mark"], ops[o["sem"]]["clock"]
+            continue
+        kn = known[q]
+        for j in sorted(o["dep"], key=lambda j: -ops[j]["end"]):
+            d = ops[j]
+            s, v = d["mark"]
+            if (q == "pe" and d["q"] == "pe") or kn.get(s, 0) >= v:
+                continue
+            eng[q].wait_ge(T.sem[s], v)
+            for s2, v2 in d["clock"].items():
+                kn[s2] = max(kn.get(s2, 0), v2)
+        res = o["emit"]()
+        s, v = o["sem"] or ("q_" + q, 1)
+        total[s] = total.get(s, 0) + v
+        if o["sem"] is None:
+            res.then_inc(T.sem[s], 1)
+        elif s != "sent":
+            for ins in res:
+                ins.then_inc(T.sem[s], 16)
+        o["mark"] = (s, total[s])
+        o["clock"] = dict(kn)
+        o["clock"][s] = total[s]
+    for s, v in total.items():
+        if max(known[q].get(s, 0) for q in known) < v:
+            (g.sync if s == "d_y" else g).wait_ge(T.sem[s], v)

@@ -10,24 +10,40 @@ W0 = A0 + N * S
 WIDTH = W0 + C
 ORDER = [0, 3, 4, 7, 1, 2, 5, 6]
 RUNS = [(0, 1), (1, 3), (3, 4), (4, 6), (6, 8)]
-FIRST = [512, 512, 512, 384, 128]
-MAIN = [(256, "f?"), (512, "f?"), (256, "saa"), (256, "saa"), (256, "saa"), (320, "f?"), (128, "f?"), (64, "f?")]
-SECOND = [(128, "f?"), (128, "f?")] + MAIN[1:]
 GIVEN = [64, 64, 96]
-LAST = [256, 512, 640, 640]
-BY_ENGINE = [9, 0, 0, 0, 2]
+TAKEN = [128, 128]
+LAST = [128, 128, 288, 288, 384, 384, 224, 224]
 MERGE = 256
+BANKS = 6
+THIRD = STEPS
 ALL16 = False
-ROUNDS = 6
-LAT = [9000, 3500]
-PLANS = [(1.0, 1.56, 0.5, 100.0), (0.9, 1.2, 0.45, 80.0), (1.15, 1.95, 0.55, 130.0)]
+FIRST = "256b 512b 512b 512b 256b"
+SECOND = "64f 256f 512f 384s 384s 256s 128s 64f"
+MAIN = "320f 512f 384s 384s 256s 128s 64f"
+STEADY = {"dve": "gC g0 aA aB g1 aC r2 r3 r4 l2 a0 r5 l3 a1 l4 a2 l5 a3 a4 a5 a6",
+          "act": "gA gB sA sB sC g2 g3 g4 p2 m2 s0 g5 p3 s1 s2 p4 p5 m5 s3 g6 s4 s5 s6",
+          "pool": "far near m3 m4"}
+QUEUES = [
+    {"dve": "ones pd0 pd1 pf dg nd sf0 sf1 su0 gA su1 gC si bo sh0 sh1 nk shu mj "
+            "a0 qm a1 rd a2 sc a3 t1 a4 t2 aZ offs",
+     "act": "fill gB wc0 wc1 wc2 wc3 wc4 s0 m1 s1 wf s2 s3 s4 sZ",
+     "pool": "pc i16 i8 ic pm far near wb"},
+    {"dve": "gA gC gt aA go aB off aC aX aY g0 g2 r3 r4 a0 a1 l3 r5 l4 r6 a2 l5 a3 l6 a4 a5 a6 a7",
+     "act": "gB sA sB sC sX sY g1 g3 g4 s0 s1 p3 g5 p4 g6 s2 s3 p5 g7 s4 p6 s5 s6 s7",
+     "pool": "far near m3 m4 m5 m6"},
+    STEADY, STEADY,
+    {"dve": STEADY["dve"] + " y0 y2 y4 y6",
+     "act": STEADY["act"] + " d3 y1 y3 y5 y7 o7",
+     "pool": STEADY["pool"] + " u3 u5 d5 u6 d6"}]
 
 SCRATCH = {"wr": ("sbuf", [128, 2, 128], "bfloat16"), "wc": ("sbuf", [128, 2, 128], "bfloat16")}
-for _d, _l in (("bfloat16", [("fl", C), ("wb", 256), ("ones", 64), ("pm", 128), ("vs0", NS), ("hi", C), ("md", C), ("lo", C)]),
+for _d, _l in (("bfloat16", [("fl", C), ("wb", 256), ("ones", 64), ("pm", 128), ("vs0", NS), ("ar0", N * S), ("hi", C),
+                             ("md", C), ("lo", C)]),
                ("float32", [("wf", 256), ("bo", 128), ("i8", 128), ("i16", NS), ("dg", NS), ("nd", NS), ("ic", 128),
                             ("nk", 128), ("mj", 16), ("pf", 4), ("sf", 16), ("gt", 128), ("go", 128), ("m1", NS),
-                            ("qm", NS), ("rd", NS), ("sc", NS), ("t1", 16), ("t2", 16), ("vf", NS + C), ("sq", NS + C),
-                            ("rr", C), ("sb", STEPS * NS)] + [("w%d" % _t, WIDTH) for _t in range(STEPS)]),
+                            ("qm", NS), ("rd", NS), ("sc", NS), ("t1", 16), ("t2", 16), ("vf", NS + C),
+                            ("sq", NS + C + N * S), ("rr", C), ("sb", STEPS * NS)]
+                + [("w%d" % _t, WIDTH) for _t in range(STEPS)]),
                ("int32", [("pc", 4), ("pd", 4), ("s16", 16), ("si", 16), ("sh", 32), ("gi", 128)]),
                ("uint16", [("su", 16), ("shu", 32), ("off", 128), ("offs", 16)])):
     for _n, _w in _l:
@@ -35,20 +51,25 @@ for _d, _l in (("bfloat16", [("fl", C), ("wb", 256), ("ones", 64), ("pm", 128), 
 for _b in range(8):
     SCRATCH["ps%d" % _b] = ("psum", [128, 512], "float32")
 
-SEMAPHORES = (["q_pe", "q_act", "q_dve", "q_pool", "sent", "d_s", "d_f", "d_w", "d_b", "d_l", "d_y"]
-              + ["arr%d" % t for t in range(STEPS)] + ["rly%d" % t for t in range(STEPS)]
-              + ["sw%d_%d" % (t, k) for t in range(STEPS) for k in range(12)])
+SEMAPHORES = (["q_pe", "q_act", "q_dve", "q_pool", "sent", "d_s", "d_f", "d_w", "d_l", "d_y", "sent_first"]
+              + [_n + "%d" % _t for _t in range(STEPS) for _n in ("arr", "rly")]
+              + ["sw%d_%d" % (_t, _k) for _t in range(STEPS) for _k in range(12)])
 
 
 def routes(T, topo, r):
     me = T.cores[r]
     far = [q for q in range(N) if q != r and not topo.may_write(me, T.cores[q])]
     near = [q for q in range(N) if q != r and q not in far]
-    able = [c for c in topo.cores_of(me)
-            if c != me and T.rank_of(c) is None and all(topo.may_write(c, T.cores[q]) for q in far)]
-    able.sort(key=lambda c: topo.die(c) != topo.die(me))
+    free = sorted((c for c in topo.cores_of(me) if c != me and T.rank_of(c) is None),
+                  key=lambda c: topo.die(c) != topo.die(me))
+    able = [c for c in free if all(topo.may_write(c, T.cores[q]) for q in far)][:2]
     half = (len(far) + 1) // 2
-    return far, near, [(able[0], far[:half]), (able[1], far[half:])]
+    return far, near, [(able[0], far[:half]), (able[1], far[half:]), ([c for c in free if c not in able][0], near[-1:])]
+
+
+def senders(T, topo, r, t):
+    far, near, relays = routes(T, topo, r)
+    return relays + [(T.cores[r], near[:-1])] if t >= THIRD else relays[:2] + [(T.cores[r], near)]
 
 
 def deal(engines, k):
@@ -65,12 +86,11 @@ def deal(engines, k):
     return out
 
 
-def arrivals(T, topo, r):
+def arrivals(T, topo, r, t):
     n = 0
     for q in range(N):
         if q != r:
-            far, near, relays = routes(T, topo, q)
-            for c, ds in relays + [(T.cores[q], near)]:
+            for c, ds in senders(T, topo, q, t):
                 if r in ds:
                     n += deal(topo.engines(c, T.cores[r]), len(ds))[ds.index(r)][1]
     return n
@@ -80,248 +100,259 @@ def inward(T, topo, r):
     me = T.cores[r]
     far, near, relays = routes(T, topo, r)
     out = topo.engines(me, T.cores[near[0]])
-    return deal([e for e in topo.engines(me, relays[0][0]) if ALL16 or e not in out], len(relays))
+    on = topo.engines(me, relays[0][0])
+    return deal([e for e in on if ALL16 or e not in out], 2) + deal([e for e in on if e not in out], 1)
+
+
+def given(T, t, at, n):
+    return T.sb[:, t * NS + at:t * NS + at + n] if t else T.vs0[:, at:at + n]
 
 
 def outward(T, topo, core, r, ds, t, at):
     tr, n = [], 0
     for i, (q, (m, k)) in enumerate(zip(ds, deal(topo.engines(core, T.cores[ds[0]]), len(ds)))):
         rid, pid = topo.addr(T.cores[q], core)
-        tr.append(RemoteDMATransfer(dst_ids=[DstId(rid=rid, pnc=pid)], dma_engine_mask=m,
-                                    remote_sem=T.sem["arr%d" % t], src=T.sb[:, at + i * S:at + (i + 1) * S],
-                                    dst=T["w%d" % t][:, A0 + r * S:A0 + (r + 1) * S]))
+        dst = T["w%d" % t][:, A0 + r * S:A0 + (r + 1) * S] if t else T.ar0[:, r * S:(r + 1) * S]
+        tr.append(RemoteDMATransfer(dst_ids=[DstId(rid=rid, pnc=pid)], dma_engine_mask=m, remote_sem=T.sem["arr%d" % t],
+                                    src=given(T, t, at + i * S, S), dst=dst))
         n += k
     return tr, n
 
 
 def relay_program(g, core, T, topo, r, k):
     total = 0
-    for t in range(STEPS):
+    for t in range(k // 2 * THIRD, STEPS):
         g.wait_ge(T.sem["rly%d" % t], inward(T, topo, r)[k][1])
-        tr, n = outward(T, topo, core, r, routes(T, topo, r)[2][k][1], t, t * NS)
+        tr, n = outward(T, topo, core, r, routes(T, topo, r)[2][k][1], t, 0)
         g.remote_dma_fused(tr, local_sem=T.sem.sent)
         total += n
-    g.wait_ge(T.sem.sent, total)
+    if total:
+        g.wait_ge(T.sem.sent, total)
 
 
 def build_ops(g, core, T, topo, r):
-    ops = []
+    ops, now = [], [0]
     V, A, P = g.vector, g.scalar, g.tensor
 
-    def op(alts, rd, wr, sem=None, lat=0.0, after=(), behind=()):
-        ops.append({"alts": alts, "rd": rd, "wr": wr, "sem": sem, "lat": lat, "after": list(after),
-                    "behind": list(behind)})
+    def op(name, alts, rd, wr, sem=None, after=()):
+        ops.append({"name": (now[0], name), "alts": alts, "rd": rd, "wr": wr, "sem": sem, "after": list(after)})
         return len(ops) - 1
 
     def R(buf, a=0, b=1 << 20, p=0, q=128):
         return (buf, a, b, p, q)
 
-    def ve(n, f, rd, wr, c=1, behind=()):
-        return op([("dve", (40, max(64, n * c), 0, 0), f)], rd, wr, behind=behind)
+    def ve(name, f, rd, wr):
+        return op(name, {"dve": f}, rd, wr)
 
-    def vg(n, f, rd, wr):
-        return op([("dve", (50, 0, n, 0), f)], rd, wr)
+    def pool(name, f, rd, wr):
+        return op(name, {"pool": f}, rd, wr)
 
-    def copy(n, out, in_, rd, wr, gather=False, only=None, behind=()):
-        cv = (50, 0, n, 0) if gather else (40, max(64, n), 0, 0)
-        ca = (65, 0, n, 0) if gather else cv
-        alts = [("dve", cv, lambda: V.tensor_copy(out, in_)), ("act", ca, lambda: A.activation(out, in_, ACT.Copy))]
-        return op([x for x in alts if only in (None, x[0])], rd, wr, behind=behind)
+    def copy(name, n, out, in_, rd, wr):
+        return op(name, {"dve": lambda: V.tensor_copy(out, in_), "act": lambda: A.activation(out, in_, ACT.Copy),
+                         "pool": lambda: g.affine_select(out, in_, [[0, n]], ALU.is_equal, 0.0, 0, 0)}, rd, wr)
 
-    def mm(n, out, lhsT, rhs, start, stop, rd, bank, wide, after=()):
-        return op([("pe", (10, 0, 0, max(64, n) * (4 if wide else 1)), lambda: P.matmul(out, lhsT, rhs, start, stop))],
-                  rd, [R(bank)], after=after)
+    def mm(out, lhsT, rhs, start, stop, rd, bank):
+        return op(None, {"pe": lambda: P.matmul(out, lhsT, rhs, start, stop)}, rd, [R(bank)])
 
-    def pool(ns, f, rd, wr):
-        return op([("pool", (ns, 0, 0, 0), f)], rd, wr)
-
-    def dma(q, pairs, sem, rd, wr, rows, size, behind=()):
-        e = g.sync if q == "sp" else g.scalar
-        x = op([(q, (60 * len(pairs), 0, 0, 0), lambda: [e.dma_start(o, i) for o, i in pairs])], rd, wr,
-               sem=(sem, 16 * len(pairs)), lat=800, behind=behind)
-        op([("dq", (rows * (40 + size / 25) / 16, 0, 0, 0), None)], [], wr, sem=x, lat=900, after=[x],
-           behind=[j + 1 for j in behind])
-        return x
+    def dma(pairs, sem, rd, wr, after=(), name=None):
+        q, e = ("act", A) if name else ("sp", g.sync)
+        return op(name, {q: lambda: [e.dma_start(o, i) for o, i in pairs]}, rd, wr, sem=(sem, 16 * len(pairs)), after=after)
 
     far, near, relays = routes(T, topo, r)
     nfar = len(far) * S
     K = NS // 16
 
-    x = dma("sp", [(T.s16[0:16, :], T.sends[:])], "d_s", [], [R("s16")], 16, 64)
-    m = dma("act", [(T.wr[:, 0, :], T.mix[:])], "d_w", [], [R("wr", 0, 1)], 128, 256)
-    x = dma("sp", [(T.wr[:, 1, :], T.bend[:])], "d_b", [], [R("wr", 1, 2)], 128, 256, [x])
-    x = dma("sp", [(T.fl[:], T.flow[:])], "d_f", [], [R("fl")], 128, 4096, [x, m])
-    dma("sp", [(T.gi[16 * a:16 * b, :], T.links[16 * ORDER[a]:16 * (ORDER[a] + b - a), :]) for a, b in RUNS],
-        "d_l", [], [R("gi")], 128, 512, [x])
+    dma([(T.s16[0:16, :], T.sends[:])], "d_s", [], [R("s16")])
+    dma([(T.fl[:], T.flow[:])], "d_f", [], [R("fl")])
+    dma([(T.wr[:, 1, :], T.bend[:]), (T.wr[:, 0, :], T.mix[:])], "d_w", [], [R("wr")])
+    dma([(T.gi[16 * a:16 * b, :], T.links[16 * ORDER[a]:16 * (ORDER[a] + b - a), :]) for a, b in RUNS],
+        "d_l", [], [R("gi")])
 
     imp = {"allow_small_or_imprecise_dtypes": True}
-    pool(140, lambda: g.iota(T.pc[:, 0:1], [[0, 1]], 0, 1), [], [R("pc")])
-    pool(560, lambda: g.iota(T.i16[:], [[0, K], [1, 16]], 0, 0, **imp), [], [R("i16")])
-    ve(1, lambda: V.tensor_scalar(T.pd[:, 0:1], T.pc[:, 0:1], 15, None, ALU.bitwise_and), [R("pc")], [R("pd", 0, 1)])
-    ve(1, lambda: V.tensor_scalar(T.pd[:, 1:2], T.pc[:, 0:1], 4, None, ALU.arith_shift_right), [R("pc")], [R("pd", 1, 2)])
-    ve(2, lambda: V.tensor_copy(T.pf[:, 0:2], T.pd[:, 0:2]), [R("pd")], [R("pf")])
-    ve(NS, lambda: V.tensor_scalar(T.dg[:], T.i16[:], T.pf[:, 0:1], None, ALU.is_equal), [R("i16"), R("pf")], [R("dg")])
-    ve(64, lambda: V.memset(T.ones[:], 1.0), [], [R("ones")])
-    for t in range(STEPS):
-        ve(S, lambda t=t: V.memset(T["w%d" % t][:, A0 + r * S:A0 + (r + 1) * S], 0.0), [],
-           [R("w%d" % t, A0 + r * S, A0 + (r + 1) * S)])
+    pool("pc", lambda: g.iota(T.pc[:, 0:1], [[0, 1]], 0, 1), [], [R("pc")])
+    pool("i16", lambda: g.iota(T.i16[:], [[0, K], [1, 16]], 0, 0, **imp), [], [R("i16")])
+    pool("i8", lambda: g.iota(T.i8[:], [[1, 8], [0, 16]], 0, 0, **imp), [], [R("i8")])
+    pool("ic", lambda: g.iota(T.ic[:], [[-16, 128]], -(W0 - H0), 0, **imp), [], [R("ic")])
+    ve("ones", lambda: V.memset(T.ones[:], 1.0), [], [R("ones")])
     for a in range(2):
         o = ORDER[4 * a:4 * a + 4]
         pat = [[-16 * (o[2] - o[0]), 2], [-16 * (o[1] - o[0]), 2], [-1, 16]]
-        pool(300, lambda a=a, o=o, pat=pat: g.affine_select(T.pm[:, 64 * a:64 * a + 64], T.ones[:], pat, ALU.is_equal,
-                                                            0.0, -16 * o[0], 1), [R("ones")], [R("pm", 64 * a, 64 * a + 64)])
-    pool(380, lambda: g.iota(T.i8[:], [[1, 8], [0, 16]], 0, 0, **imp), [], [R("i8")])
-    pool(380, lambda: g.iota(T.ic[:], [[-16, 128]], -(W0 - H0), 0, **imp), [], [R("ic")])
+        pool("pm", lambda a=a, o=o, pat=pat: g.affine_select(T.pm[:, 64 * a:64 * a + 64], T.ones[:], pat, ALU.is_equal,
+                                                             0.0, -16 * o[0], 1), [R("ones")], [R("pm", 64 * a, 64 * a + 64)])
+    ve("pd0", lambda: V.tensor_scalar(T.pd[:, 0:1], T.pc[:, 0:1], 15, None, ALU.bitwise_and), [R("pc")], [R("pd", 0, 1)])
+    ve("pd1", lambda: V.tensor_scalar(T.pd[:, 1:2], T.pc[:, 0:1], 4, None, ALU.arith_shift_right), [R("pc")], [R("pd", 1, 2)])
+    ve("pf", lambda: V.tensor_copy(T.pf[:, 0:2], T.pd[:, 0:2]), [R("pd")], [R("pf")])
+    ve("dg", lambda: V.tensor_scalar(T.dg[:], T.i16[:], T.pf[:, 0:1], None, ALU.is_equal), [R("i16"), R("pf")], [R("dg")])
+    ve("nd", lambda: V.tensor_scalar(T.nd[:], T.i16[:], T.pf[:, 0:1], None, ALU.not_equal), [R("i16"), R("pf")], [R("nd")])
+    ve("bo", lambda: V.tensor_scalar(T.bo[:], T.i8[:], T.pf[:, 1:2], None, ALU.is_equal), [R("i8"), R("pf")], [R("bo")])
+    ve("nk", lambda: V.tensor_scalar(T.nk[:], T.ic[:], T.pf[:, 0:1], None, ALU.subtract), [R("ic"), R("pf")], [R("nk")])
+    ve("mj", lambda: V.tensor_scalar(T.mj[:], T.nk[:, 0:16], float(W0 - H0 + NS), None, ALU.add), [R("nk")], [R("mj")])
+    for buf, a in [("ar0", r * S)] + [("w%d" % t, A0 + r * S) for t in range(1, STEPS)]:
+        copy("fill", S, T[buf][:, a:a + S], T.ones[:, 0:S], [R("ones")], [R(buf, a, a + S)])
 
-    runs = []
-    for i, q in enumerate(far + near):
-        if runs and runs[-1][1] + runs[-1][2] == q:
-            runs[-1][2] += 1
-        else:
-            runs.append([i, q, 1])
-    for i, q, n in runs:
-        ve(2 * n, lambda i=i, q=q, n=n: V.tensor_copy(T.sf[0:16, 2 * i:2 * (i + n)], T.s16[0:16, 2 * q:2 * (q + n)]),
-           [R("s16")], [R("sf", 2 * i, 2 * (i + n))])
-    mm(K, T.ps6[:, 0:K], T.dg[0:16, 0:128], T.sf[0:16, 0:K], True, True, [R("dg"), R("sf")], "ps6", True)
-    ve(K, lambda: V.tensor_copy(T.su[:, 0:K], T.ps6[:, 0:K]), [R("ps6")], [R("su")])
-    ve(K, lambda: V.tensor_copy(T.si[:, 0:K], T.ps6[:, 0:K]), [R("ps6")], [R("si")])
+    for k, (at, ds) in enumerate(((0, far), (len(far), near))):
+        runs = []
+        for i, q in enumerate(ds):
+            if runs and runs[-1][1] + runs[-1][2] == q:
+                runs[-1][2] += 1
+            else:
+                runs.append([at + i, q, 1])
+        for i, q, n in runs:
+            ve("sf%d" % k, lambda i=i, q=q, n=n: V.tensor_copy(T.sf[0:16, 2 * i:2 * (i + n)], T.s16[0:16, 2 * q:2 * (q + n)]),
+               [R("s16")], [R("sf", 2 * i, 2 * (i + n))])
+        a, b, bank = 2 * at, 2 * (at + len(ds)), "ps%d" % (6 + k)
+        mm(T[bank][:, a:b], T.dg[0:16, 0:128], T.sf[0:16, a:b], True, True, [R("dg"), R("sf", a, b)], bank)
+        ve("su%d" % k, lambda a=a, b=b, bank=bank: V.tensor_copy(T.su[:, a:b], T[bank][:, a:b]), [R(bank)], [R("su", a, b)])
+    ve("si", lambda: V.tensor_copy(T.si[:, 0:K], T.su[:, 0:K]), [R("su")], [R("si")])
+    ve("sh0", lambda: V.tensor_scalar(T.sh[:, 0:K], T.si[:, 0:K], 4, None, ALU.arith_shift_right), [R("si")], [R("sh", 0, K)])
+    ve("sh1", lambda: V.tensor_scalar(T.sh[:, K:2 * K], T.si[:, 0:K], 15, None, ALU.bitwise_and), [R("si")], [R("sh", K, 2 * K)])
+    ve("shu", lambda: V.tensor_copy(T.shu[:, 0:2 * K], T.sh[:, 0:2 * K]), [R("sh")], [R("shu")])
 
-    for a, b in RUNS:
-        x = 16 * ORDER[a]
-        op([("act", (40, 64, 0, 0), lambda a=a, b=b, x=x: A.activation(
-            T.wc[:, :, 16 * a:16 * b], T.wr[:, :, x:x + 16 * (b - a)], ACT.Copy))], [R("wr")], [R("wc", 16 * a, 16 * b)])
+    for k, (a, b) in enumerate(RUNS):
+        c = 16 * ORDER[a]
+        copy("wc%d" % k, 0, T.wc[:, :, 16 * a:16 * b], T.wr[:, :, c:c + 16 * (b - a)], [R("wr")], [R("wc", 16 * a, 16 * b)])
 
-    def late_setup(x):
-        m0 = mm(128, T.ps7[:, 0:128], T.pm[:], T.wc[:, 0, :], True, True, [R("pm"), R("wc")], "ps7", False)
-        mm(128, T.ps7[:, 128:256], T.pm[:], T.wc[:, 1, :], True, True, [R("pm"), R("wc")], "ps7", False, after=[m0])
-        copy(256, T.wf[:], T.ps7[:, 0:256], [R("ps7")], [R("wf")])
-        copy(256, T.wb[:], T.wf[:], [R("wf")], [R("wb")])
-        ve(NS, lambda: V.tensor_scalar(T.nd[:], T.i16[:], T.pf[:, 0:1], None, ALU.not_equal), [R("i16"), R("pf")], [R("nd")], behind=x)
-        ve(128, lambda: V.tensor_scalar(T.bo[:], T.i8[:], T.pf[:, 1:2], None, ALU.is_equal), [R("i8"), R("pf")], [R("bo")], behind=x)
-        ve(128, lambda: V.tensor_scalar(T.nk[:], T.ic[:], T.pf[:, 0:1], None, ALU.subtract), [R("ic"), R("pf")], [R("nk")], behind=x)
-        ve(16, lambda: V.tensor_scalar(T.mj[:], T.nk[:, 0:16], float(W0 - H0 + NS), None, ALU.add), [R("nk")], [R("mj")])
-        ve(128, lambda: V.tensor_tensor(T.gt[:], T.gi[:], T.nk[:], ALU.mult), [R("gi"), R("nk")], [R("gt")], 2)
-        ve(128, lambda: V.tensor_tensor(T.go[:], T.gi[:], T.gt[:], ALU.max), [R("gi"), R("gt")], [R("go")], 2)
-        ve(128, lambda: V.tensor_copy(T.off[:], T.go[:]), [R("go")], [R("off")])
-        ve(K, lambda: V.tensor_scalar(T.sh[:, 0:K], T.si[:, 0:K], 4, None, ALU.arith_shift_right), [R("si")], [R("sh", 0, K)], behind=x)
-        ve(K, lambda: V.tensor_scalar(T.sh[:, K:2 * K], T.si[:, 0:K], 15, None, ALU.bitwise_and), [R("si")], [R("sh", K, 2 * K)], behind=x)
-        ve(2 * K, lambda: V.tensor_copy(T.shu[:, 0:2 * K], T.sh[:, 0:2 * K]), [R("sh")], [R("shu")])
-        copy(NS, T.m1[:], T.dg[:, 0:16].indirect(T.shu[:, K:2 * K]), [R("dg"), R("shu")], [R("m1")], gather=True)
-        vg(NS, lambda: V.tensor_tensor(T.qm[:], T.gi[:, 0:128].indirect(T.shu[:, 0:K]), T.m1[:], ALU.mult),
+    def rows_of_weights():
+        mm(T.ps6[:, 0:128], T.pm[:], T.wc[:, 0, :], True, True, [R("pm"), R("wc")], "ps6")
+        mm(T.ps6[:, 128:256], T.pm[:], T.wc[:, 1, :], True, True, [R("pm"), R("wc")], "ps6")
+        copy("wf", 256, T.wf[:], T.ps6[:, 0:256], [R("ps6")], [R("wf")])
+        copy("wb", 256, T.wb[:], T.wf[:], [R("wf")], [R("wb")])
+
+    def offsets():
+        now[0] = 1
+        ve("gt", lambda: V.tensor_tensor(T.gt[:], T.gi[:], T.nk[:], ALU.mult), [R("gi"), R("nk")], [R("gt")])
+        ve("go", lambda: V.tensor_tensor(T.go[:], T.gi[:], T.gt[:], ALU.max), [R("gi"), R("gt")], [R("go")])
+        ve("off", lambda: V.tensor_copy(T.off[:], T.go[:]), [R("go")], [R("off")])
+        now[0] = 0
+        copy("m1", NS, T.m1[:], T.dg[:, 0:16].indirect(T.shu[:, K:2 * K]), [R("dg"), R("shu")], [R("m1")])
+        ve("qm", lambda: V.tensor_tensor(T.qm[:], T.gi[:, 0:128].indirect(T.shu[:, 0:K]), T.m1[:], ALU.mult),
            [R("gi"), R("shu"), R("m1")], [R("qm")])
-        mm(NS, T.ps7[:, 0:NS], T.bo[:], T.qm[:], True, True, [R("bo"), R("qm")], "ps7", True)
-        ve(NS, lambda: V.tensor_tensor(T.rd[:], T.ps7[:, 0:NS], T.dg[:], ALU.mult), [R("ps7"), R("dg")], [R("rd")])
-        ve(NS, lambda: V.tensor_tensor_scan(T.sc[:], T.nd[:], T.rd[:], 0.0, ALU.mult, ALU.add), [R("nd"), R("rd")], [R("sc")])
-        ve(K, lambda: V.tensor_tensor(T.t1[:, 0:K], T.sc[:, 15:NS:16], T.mj[:, 0:K], ALU.mult), [R("sc"), R("mj")], [R("t1")])
-        ve(K, lambda: V.tensor_tensor(T.t2[:, 0:K], T.sc[:, 15:NS:16], T.t1[:, 0:K], ALU.min), [R("sc"), R("t1")], [R("t2")])
-        ve(K, lambda: V.tensor_scalar(T.offs[:, 0:K], T.t2[:, 0:K], float(NS), None, ALU.add), [R("t2")], [R("offs")])
+        mm(T.ps7[:, 0:NS], T.bo[:], T.qm[:], True, True, [R("bo"), R("qm")], "ps7")
+        ve("rd", lambda: V.tensor_tensor(T.rd[:], T.ps7[:, 0:NS], T.dg[:], ALU.mult), [R("ps7"), R("dg")], [R("rd")])
+        ve("sc", lambda: V.tensor_tensor_scan(T.sc[:], T.nd[:], T.rd[:], 0.0, ALU.mult, ALU.add), [R("nd"), R("rd")], [R("sc")])
+        ve("t1", lambda: V.tensor_tensor(T.t1[:, 0:K], T.sc[:, 15:NS:16], T.mj[:, 0:K], ALU.mult), [R("sc"), R("mj")], [R("t1")])
+        ve("t2", lambda: V.tensor_tensor(T.t2[:, 0:K], T.sc[:, 15:NS:16], T.t1[:, 0:K], ALU.min), [R("sc"), R("t1")], [R("t2")])
+        ve("offs", lambda: V.tensor_scalar(T.offs[:, 0:K], T.t2[:, 0:K], float(NS), None, ALU.add), [R("t2")], [R("offs")])
 
-    chain = []
-    who = {"a": "act", "v": "dve", "?": None}
+    turn = [0]
     root = math.sqrt(0.125)
 
-    def collide(n, pieces, wbuf, x, out, outr):
-        k = len(chain) % 4
-        ba, bb = "ps%d" % (2 * k), "ps%d" % (2 * k + 1)
-        pa, pb = T[ba][:, 0:n], T[bb][:, 0:n]
-        wm, wbd = (T.wc[:, 0, :], T.wc[:, 1, :]) if wbuf == "wc" else (T[wbuf][:, 0:128], T[wbuf][:, 128:256])
-        last = chain[-1:]
-        for i, (ap, reg) in enumerate(pieces):
-            st, sp = i == 0, i == len(pieces) - 1
-            last = [mm(n, pb, wbd, ap, st, sp, [R(wbuf), reg], bb, wbuf == "wf", after=last)]
-            last = [mm(n, pa, wm, ap, st, sp, [R(wbuf), reg], ba, wbuf == "wf", after=last)]
-        chain.append(last[0])
-        op([("act", (40, max(64, n), 0, 0), lambda: A.activation(T.sq[:, x:x + n], pb, ACT.Square, scale=root))],
+    def collide(k, n, pieces, wbuf, x, out, outr, swapped=False):
+        ba, bb = "ps%d" % (turn[0] % BANKS), "ps%d" % (turn[0] % BANKS + 1)
+        turn[0] += 2
+        for j, bank in ((1, bb), (0, ba)):
+            for i, (ap, reg) in enumerate(pieces):
+                for p, q, z in ((0, 64, 64), (64, 128, 0)) if swapped else ((0, 128, 0),):
+                    w = T.wc[:, j, z:z + q - p] if wbuf == "wc" else T[wbuf][:, 128 * j:128 * j + 128]
+                    mm(T[bank][p:q, 0:n], w, ap, i == 0, i == len(pieces) - 1, [R(wbuf), reg], bank)
+        op("s" + k, {"act": lambda: A.activation(T.sq[:, x:x + n], T[bb][:, 0:n], ACT.Square, scale=root)},
            [R(bb)], [R("sq", x, x + n)])
-        return ve(n, lambda: V.tensor_tensor(out, pa, T.sq[:, x:x + n], ALU.add), [R(ba), R("sq", x, x + n)], [outr])
+        ve("a" + k, lambda: V.tensor_tensor(out, T[ba][:, 0:n], T.sq[:, x:x + n], ALU.add), [R(ba), R("sq", x, x + n)], [outr])
 
-    def swap(sname, a, n, wn, b, sem, engine):
+    def swap(sname, a, n, wn, b, sem, k=None, after=()):
         src = T[sname]
-        if engine:
-            for p in (0, 64):
-                copy(n, T[wn][64 - p:128 - p, b:b + n], src[p:p + 64, a:a + n], [R(sname, a, a + n)],
-                     [R(wn, b, b + n, 64 - p, 128 - p)])
+        if k is None:
+            dma([(T[wn][64:128, b:b + n], src[0:64, a:a + n]), (T[wn][0:64, b:b + n], src[64:128, a:a + n])],
+                sem, [R(sname, a, a + n)], [R(wn, b, b + n)], after)
         else:
-            dma("sp", [(T[wn][64:128, b:b + n], src[0:64, a:a + n]), (T[wn][0:64, b:b + n], src[64:128, a:a + n])],
-                sem, [R(sname, a, a + n)], [R(wn, b, b + n)], 128, 4 * n)
+            for name, p in (("d", 0), ("u", 64)):
+                copy(name + k, n, T[wn][64 - p:128 - p, b:b + n], src[p:p + 64, a:a + n], [R(sname, a, a + n)],
+                     [R(wn, b, b + n, 64 - p, 128 - p)])
 
     def call(t, part):
-        if part == 0:
-            tr, n, at = [], 0, t * NS
-            for (c, ds), (m, k) in zip(relays, inward(T, topo, r)):
-                rid, pid = topo.addr(c, core)
-                wd = len(ds) * S
-                tr.append(RemoteDMATransfer(dst_ids=[DstId(rid=rid, pnc=pid)], dma_engine_mask=m,
-                                            remote_sem=T.sem["rly%d" % t], src=T.sb[:, at:at + wd],
-                                            dst=T.sb[:, t * NS:t * NS + wd]))
-                at += wd
-                n += k
-        else:
-            tr, n = outward(T, topo, core, r, near, t, t * NS + nfar)
+        tr, n = outward(T, topo, core, r, senders(T, topo, r, t)[-1][1], t, nfar) if part else ([], 0)
+        for (c, ds), (m, k) in list(zip(relays, inward(T, topo, r)))[2 * part:2 + (t >= THIRD) * part]:
+            rid, pid = topo.addr(c, core)
+            at, wd = (far + near).index(ds[0]) * S, len(ds) * S
+            tr.append(RemoteDMATransfer(dst_ids=[DstId(rid=rid, pnc=pid)], dma_engine_mask=m,
+                                        remote_sem=T.sem["rly%d" % t], src=given(T, t, at, wd), dst=given(T, t, 0, wd)))
+            n += k
         a, b = (0, nfar) if part == 0 else (nfar, NS)
-        return op([("pool", (3000 if t + part == 0 else 900, 0, 0, 0), lambda: g.remote_dma_fused(tr, local_sem=T.sem.sent))],
-                  [R("sb", t * NS + a, t * NS + b)], [], sem=("sent", n), lat=3000)
+        sem = "sent" if t + part else "sent_first"
+        return op(("far", "near")[part], {"pool": lambda: g.remote_dma_fused(tr, local_sem=T.sem[sem])},
+                  [R("sb", t * NS + a, t * NS + b) if t else R("vs0", a, b)], [], sem=(sem, n))
 
-    narr = arrivals(T, topo, r)
     for t in range(STEPS):
+        now[0] = t
         wn, wp = "w%d" % t, "w%d" % (t - 1)
+        listed = " ".join(QUEUES[t].values()).split()
         calls, b = [], 0
-        for n in GIVEN:
+        for k, n in zip("ABC", GIVEN):
             a, b = b, b + n
             x = t * NS + a
             if t == 0:
-                copy(n, T.vs0[:, a:b], T.fl[:, 0:C].indirect(T.su[:, a // 16:b // 16]), [R("fl"), R("su")],
-                     [R("vs0", a, b)], gather=True)
-                done = collide(n, [(T.vs0[:, a:b], R("vs0", a, b))], "wc", a, T.sb[:, x:x + n], R("sb", x, x + n))
+                copy("g" + k, n, T.vs0[:, a:b], T.fl[:, 0:C].indirect(T.su[:, a // 16:b // 16]), [R("fl"), R("su", a // 16, b // 16)],
+                     [R("vs0", a, b)])
             else:
-                copy(n, T.vf[:, a:b], T[wp][:, 0:A0].indirect(T.offs[:, a // 16:b // 16]),
-                     [R(wp, 0, A0), R("offs")], [R("vf", a, b)], gather=True)
-                collide(n, [(T.vf[:, a:b], R("vf", a, b))], "wf", a, T.sb[:, x:x + n], R("sb", x, x + n))
+                copy("g" + k, n, T.vf[:, a:b], T[wp][:, 0:A0].indirect(T.offs[:, a // 16:b // 16]),
+                     [R(wp, 0, A0), R("offs")], [R("vf", a, b)])
+                collide(k, n, [(T.vf[:, a:b], R("vf", a, b))], "wf", a, T.sb[:, x:x + n], R("sb", x, x + n))
             calls += [call(t, part) for part, e in enumerate((nfar, NS)) if e == b]
-        if t < STEPS - 1:
-            swap("sb", t * NS, NS, wn, 0, "sw%d_11" % t, BY_ENGINE[t] > 8)
-        blocks = [R(wn, A0 + q * S, A0 + (q + 1) * S) for q in range(N) if q != r]
-        op([(None, (0, 0, 0, 0), None)], [], blocks, sem=("arr%d" % t, narr), lat=LAT[min(t, 1)], after=calls)
+        if 0 < t < STEPS - 1:
+            swap("sb", t * NS, NS, wn, 0, "sw%d_11" % t)
+        blocks = [R(wn, A0 + q * S, A0 + (q + 1) * S) if t else R("ar0", q * S, (q + 1) * S) for q in range(N) if q != r]
+        op(None, {None: None}, [], blocks, sem=("arr%d" % t, arrivals(T, topo, r, t)))
+        if t == 1:
+            b = 0
+            for k, n in zip("XY", TAKEN):
+                a, b = b, b + n
+                collide(k, n, [(T.ar0[:, a:b], R("ar0", a, b))], "wc", NS + C + a, T[wp][:, A0 + a:A0 + b],
+                        R(wp, A0 + a, A0 + b))
         c0 = s0 = 0
-        chunks = [(n, "b") for n in FIRST] if t == 0 else SECOND if t == 1 else MAIN
-        for k, (n, mode) in enumerate(chunks):
+        chunks = (FIRST, SECOND, MAIN)[min(t, 2)].split()
+        for j, spec in enumerate(chunks):
+            k, n, mode = str(j), int(spec[:-1]), spec[-1]
             c1, x = c0 + n, NS + c0
             out, outr = T[wn][:, H0 + c0:H0 + c1], R(wn, H0 + c0, H0 + c1)
             if mode != "b":
                 src = T[wp][:, H0:W0 + c1].indirect(T.off[:, c0 // 16:c1 // 16])
                 rd = [R(wp, H0, W0 + c1), R("off")]
             if mode == "b":
-                collide(n, [(T.fl[:, c0:c1], R("fl"))], "wc", x, out, outr)
-            elif mode[0] == "f":
-                copy(n, T.vf[:, x:x + n], src, rd, [R("vf", x, x + n)], gather=True, only=who[mode[1]])
-                collide(n, [(T.vf[:, x:x + n], R("vf", x, x + n))], "wf", x, out, outr)
+                collide(k, n, [(T.fl[:, c0:c1], R("fl"))], "wc", x, out, outr)
+            elif mode == "f":
+                copy("g" + k, n, T.vf[:, x:x + n], src, rd, [R("vf", x, x + n)])
+                collide(k, n, [(T.vf[:, x:x + n], R("vf", x, x + n))], "wf", x, out, outr)
+                if c1 == C:
+                    ops[-4]["early"] = 3 if chunks[-2][-1] == "s" else 1
             else:
                 hi, md, lo, rr = T.hi[:, c0:c1], T.md[:, c0:c1], T.lo[:, c0:c1], T.rr[:, c0:c1]
-                copy(n, hi, src, rd, [R("hi", c0, c1)], gather=True, only=who[mode[1]])
-                vg(n, lambda rr=rr, src=src, hi=hi: V.tensor_tensor(rr, src, hi, ALU.subtract),
+                copy("g" + k, n, hi, src, rd, [R("hi", c0, c1)])
+                ve("r" + k, lambda rr=rr, src=src, hi=hi: V.tensor_tensor(rr, src, hi, ALU.subtract),
                    rd + [R("hi", c0, c1)], [R("rr", c0, c1)])
-                copy(n, md, rr, [R("rr", c0, c1)], [R("md", c0, c1)], only=who[mode[2]])
-                ve(n, lambda lo=lo, rr=rr, md=md: V.tensor_tensor(lo, rr, md, ALU.subtract),
-                   [R("rr", c0, c1), R("md", c0, c1)], [R("lo", c0, c1)], 2)
-                collide(n, [(hi, R("hi", c0, c1)), (md, R("md", c0, c1)), (lo, R("lo", c0, c1))], "wb", x, out, outr)
-            left = len(chunks) - k
-            if c1 - s0 >= MERGE or left <= BY_ENGINE[t] + 1:
-                swap(wn, H0 + s0, c1 - s0, wn, W0 + s0, "sw%d_%d" % (t, k), left <= BY_ENGINE[t])
+                copy("m" + k, n, md, rr, [R("rr", c0, c1)], [R("md", c0, c1)])
+                rp, reg = rr, R("rr", c0, c1)
+                if "p" + k in listed:
+                    bank = "ps%d" % (6 + j % 2)
+                    rp, reg = T[bank][:, 0:n], R(bank)
+                    copy("p" + k, n, rp, rr, [R("rr", c0, c1)], [reg])
+                ve("l" + k, lambda lo=lo, rp=rp, md=md: V.tensor_tensor(lo, rp, md, ALU.subtract),
+                   [reg, R("md", c0, c1)], [R("lo", c0, c1)])
+                collide(k, n, [(hi, R("hi", c0, c1)), (md, R("md", c0, c1)), (lo, R("lo", c0, c1))], "wb", x, out, outr)
+            if "u" + k in listed:
+                swap(wn, H0 + c0, n, wn, W0 + c0, None, k)
+                s0 = c1
+            elif c1 - s0 >= MERGE or c1 == C or "u%d" % (j + 1) in listed:
+                swap(wn, H0 + s0, c1 - s0, wn, W0 + s0, "sw%d_%d" % (t, j), None, calls[:1] if t == 0 else ())
                 s0 = c1
             c0 = c1
-            if t == 0 and k == 1:
-                late_setup([done])
+            if t == 0 and j in (1, 2):
+                (rows_of_weights, offsets)[j - 1]()
+        if t == 0:
+            collide("Z", NS, [(T.vs0[:], R("vs0"))], "wc", 0, T[wn][:, 0:NS], R(wn, 0, NS), swapped=True)
 
     wp = "w%d" % (STEPS - 1)
-    c0, x = 0, []
-    for n in LAST:
-        c1, h = c0 + n, n // 2
-        for a in (c0, c0 + h):
-            copy(h, T.vf[:, NS + a:NS + a + h], T[wp][:, H0:W0 + a + h].indirect(T.off[:, a // 16:(a + h) // 16]),
-                 [R(wp, H0, W0 + a + h), R("off")], [R("vf", NS + a, NS + a + h)], gather=True)
-        x = [dma("sp", [(T.y[16 * ORDER[a]:16 * (ORDER[a] + b - a), c0:c1], T.vf[16 * a:16 * b, NS + c0:NS + c1])
-                        for a, b in RUNS], "d_y", [R("vf", NS + c0, NS + c1)], [], 128, 4 * n, x)]
-        c0 = c1
+    b = 0
+    for k, n in enumerate(LAST):
+        a, b = b, b + n
+        copy("y%d" % k, n, T.vf[:, NS + a:NS + b], T[wp][:, H0:W0 + b].indirect(T.off[:, a // 16:b // 16]),
+             [R(wp, H0, W0 + b), R("off")], [R("vf", NS + a, NS + b)])
+        if k % 2:
+            a -= LAST[k - 1]
+            pairs = [(T.y[16 * ORDER[i]:16 * (ORDER[i] + j - i), a:b], T.vf[16 * i:16 * j, NS + a:NS + b]) for i, j in RUNS]
+            cut = 3 if "o%d" % k in listed else len(RUNS)
+            dma(pairs[:cut], "d_y", [R("vf", NS + a, NS + b)], [])
+            if pairs[cut:]:
+                dma(pairs[cut:], "d_y", [R("vf", NS + a, NS + b)], [], name="o%d" % k)
     return ops
 
 
@@ -339,98 +370,23 @@ def order_ops(ops):
             if w:
                 lst[:] = [e for e in lst if not (x[1] <= e[1][1] and e[1][2] <= x[2] and x[3] <= e[1][3] and e[1][4] <= x[4])]
             lst.append((i, x, w))
-        o["dep"] = sorted(dep)
-    n = len(ops)
-    pre = [[(j, 1) for j in o["dep"]] + [(j, 0) for j in o["behind"]] for o in ops]
-    post = [[] for o in ops]
-    for i in range(n):
-        for j, w in pre[i]:
-            post[j].append((i, w))
-
-    def ns(c, p):
-        return c[0] + (c[1] + c[2] * p[1]) * p[0] + c[3] * p[2]
-
-    def place(busy, q, t, cost):
-        for s, e in busy.get(q, []):
-            if t + cost <= s:
-                break
-            t = max(t, e)
-        return t
-
-    def take(busy, q, t, cost):
-        if q is not None:
-            busy.setdefault(q, []).append((t, t + cost))
-            busy[q].sort()
-
-    def forward(seq, p, bias):
-        busy, st, en, pick = {}, [0.0] * n, [0.0] * n, [0] * n
-        for i in seq:
-            best = None
-            for a, (q, c, emit) in enumerate(ops[i]["alts"]):
-                cost, t = ns(c, p), 0.0
-                for j, w in pre[i]:
-                    qj = ops[j]["alts"][pick[j]][0]
-                    t = max(t, en[j] + (0.0 if q == qj == "pe" else p[3]) if w else en[j] - ops[j]["lat"])
-                t = place(busy, q, t, cost)
-                key = t + cost + (bias if q == "dve" else 0.0)
-                if best is None or key < best[0]:
-                    best = (key, a, t, cost, q)
-            pick[i], st[i], en[i] = best[1], best[2], best[2] + best[3] + ops[i]["lat"]
-            take(busy, best[4], best[2], best[3])
-        return st, en, pick
-
-    def backward(en, pick, p):
-        busy, fin = {}, [0.0] * n
-        for i in sorted(range(n), key=lambda i: (-en[i], -i)):
-            q, c, emit = ops[i]["alts"][pick[i]]
-            cost, t = ns(c, p), ops[i]["lat"]
-            for j, w in post[i]:
-                qj = ops[j]["alts"][pick[j]][0]
-                t = max(t, fin[j] + ops[i]["lat"] + (0.0 if q == qj == "pe" else p[3]) if w else fin[j])
-            t = place(busy, q, t, cost)
-            fin[i] = t + cost
-            take(busy, q, t, cost)
-        return fin
-
-    def replay(seq, pick, p):
-        free, en = {}, [0.0] * n
-        for i in seq:
-            q, c, emit = ops[i]["alts"][pick[i]]
-            t = free.get(q, 0.0)
-            for j, w in pre[i]:
-                if w:
-                    t = max(t, en[j] + (0.0 if q == ops[j]["alts"][pick[j]][0] == "pe" else p[3]))
-            if q is not None:
-                free[q] = t + ns(c, p)
-            en[i] = t + ns(c, p) + ops[i]["lat"]
-        return max(en)
-
-    def legal(key):
-        for i in range(n - 1, -1, -1):
-            for j, w in pre[i]:
-                key[j] = max(key[j], key[i])
-        return sorted(range(n), key=lambda i: (-key[i], i))
-
-    best, seed, p = None, 12345, PLANS[0]
-    for bias in (0.0, 150.0, 400.0):
-        key = [0.0] * n
-        for i in range(n - 1, -1, -1):
-            key[i] += min(ns(a[1], p) for a in ops[i]["alts"]) + ops[i]["lat"] + p[3]
-            for j, w in pre[i]:
-                key[j] = max(key[j], key[i])
-        for rnd in range(ROUNDS):
-            st, en, pick = forward(legal(key), p, bias)
-            seq = sorted(range(n), key=lambda i: (st[i], i))
-            score = sum(replay(seq, pick, x) for x in PLANS)
-            if best is None or score < best[0]:
-                best = (score, seq, en, pick)
-            key = backward(en, pick, p)
-            for i in range(n):
-                seed = (seed * 1103515245 + 12345) % 2147483648
-                key[i] += 200.0 * (rnd % 3) * seed / 2147483648
-    score, seq, en, pick = best
+        o["dep"] = dep
+    lines = {}
     for i, o in enumerate(ops):
-        o["q"], o["emit"], o["end"] = o["alts"][pick[i]][0], o["alts"][pick[i]][2], en[i]
+        if o["name"][1] is None:
+            line = lines.setdefault(list(o["alts"])[0], [])
+            line.insert(len(line) - o.get("early", 0), i)
+    for t, queues in enumerate(QUEUES):
+        for q, names in queues.items():
+            for name in names.split():
+                lines.setdefault(q, []).extend(i for i, o in enumerate(ops) if o["name"] == (t, name))
+    seq, done = [], set()
+    while len(seq) < len(ops):
+        q = [q for q, line in lines.items() if line and ops[line[0]]["dep"] <= done][0]
+        i = lines[q].pop(0)
+        ops[i]["q"] = q
+        seq.append(i)
+        done.add(i)
     return seq
 
 
@@ -453,11 +409,8 @@ def rank_program(g, core, T, topo):
             o["mark"], o["clock"] = o["sem"], {o["sem"][0]: o["sem"][1]}
             total[o["sem"][0]] = o["sem"][1]
             continue
-        if q == "dq":
-            o["mark"], o["clock"] = ops[o["sem"]]["mark"], ops[o["sem"]]["clock"]
-            continue
         kn = known[q]
-        for j in sorted(o["dep"], key=lambda j: -ops[j]["end"]):
+        for j in sorted(o["dep"], reverse=True):
             d = ops[j]
             s, v = d["mark"]
             if (q == "pe" and d["q"] == "pe") or kn.get(s, 0) >= v:
@@ -465,12 +418,12 @@ def rank_program(g, core, T, topo):
             eng[q].wait_ge(T.sem[s], v)
             for s2, v2 in d["clock"].items():
                 kn[s2] = max(kn.get(s2, 0), v2)
-        res = o["emit"]()
+        res = o["alts"][q]()
         s, v = o["sem"] or ("q_" + q, 1)
         total[s] = total.get(s, 0) + v
         if o["sem"] is None:
             res.then_inc(T.sem[s], 1)
-        elif s != "sent":
+        elif q != "pool":
             for ins in res:
                 ins.then_inc(T.sem[s], 16)
         o["mark"] = (s, total[s])

import math
from concourse.bass import DstId, RemoteDMATransfer
from concourse.mybir import AluOpType as ALU, ActivationFunctionType as ACT

C, S, N, STEPS = 2048, 32, 8, 5
NS = (N - 1) * S
H0 = NS
A0 = H0 + C
W0 = A0 + N * S
WIDTH = W0 + C
ORDER = [0, 3, 4, 7, 1, 2, 5, 6]
RUNS = [(0, 1), (1, 3), (3, 4), (4, 6), (6, 8)]
GIVEN = [64, 64, 96]
TAKEN = [128, 128]
LAST = [128, 128, 288, 288, 384, 384, 224, 224]
MERGE = 256
BANKS = 6
THIRD = STEPS
ALL16 = False
FIRST = "256b 512b 512b 512b 256b"
SECOND = "64f 256f 512f 384s 384s 256s 128s 64f"
MAIN = "320f 512f 384s 384s 256s 128s 64f"
STEADY = {"dve": "gC g0 aA aB g1 aC r2 r3 r4 l2 a0 r5 l3 a1 l4 a2 l5 a3 a4 a5 a6",
          "act": "gA gB sA sB sC g2 g3 g4 p2 m2 s0 g5 p3 s1 s2 p4 p5 m5 s3 g6 s4 s5 s6",
          "pool": "far near m3 m4"}
QUEUES = [
    {"dve": "ones pd0 pd1 pf dg nd sf0 sf1 su0 gA su1 gC si bo sh0 sh1 nk shu mj "
            "a0 qm a1 rd a2 sc a3 t1 a4 t2 aZ offs",
     "act": "fill gB wc0 wc1 wc2 wc3 wc4 s0 m1 s1 wf s2 s3 s4 sZ",
     "pool": "pc i16 i8 ic pm far near wb"},
    {"dve": "gA gC gt aA go aB off aC aX aY g0 g2 r3 r4 a0 a1 l3 r5 l4 r6 a2 l5 a3 l6 a4 a5 a6 a7",
     "act": "gB sA sB sC sX sY g1 g3 g4 s0 s1 p3 g5 p4 g6 s2 s3 p5 g7 s4 p6 s5 s6 s7",
     "pool": "far near m3 m4 m5 m6"},
    STEADY, STEADY,
    {"dve": STEADY["dve"] + " y0 y2 y4 y6",
     "act": STEADY["act"] + " d3 y1 y3 y5 y7 o7",
     "pool": STEADY["pool"] + " u3 u5 d5 u6 d6"}]

SCRATCH = {"wr": ("sbuf", [128, 2, 128], "bfloat16"), "wc": ("sbuf", [128, 2, 128], "bfloat16")}
for _d, _l in (("bfloat16", [("fl", C), ("wb", 256), ("ones", 64), ("pm", 128), ("vs0", NS), ("ar0", N * S), ("hi", C),
                             ("md", C), ("lo", C)]),
               ("float32", [("wf", 256), ("bo", 128), ("i8", 128), ("i16", NS), ("dg", NS), ("nd", NS), ("ic", 128),
                            ("nk", 128), ("mj", 16), ("pf", 4), ("sf", 16), ("gt", 128), ("go", 128), ("m1", NS),
                            ("qm", NS), ("rd", NS), ("sc", NS), ("t1", 16), ("t2", 16), ("vf", NS + C),
                            ("sq", NS + C + N * S), ("rr", C), ("sb", STEPS * NS)]
                + [("w%d" % _t, WIDTH) for _t in range(STEPS)]),
               ("int32", [("pc", 4), ("pd", 4), ("s16", 16), ("si", 16), ("sh", 32), ("gi", 128)]),
               ("uint16", [("su", 16), ("shu", 32), ("off", 128), ("offs", 16)])):
    for _n, _w in _l:
        SCRATCH[_n] = ("sbuf", [128, _w], _d)
for _b in range(8):
    SCRATCH["ps%d" % _b] = ("psum", [128, 512], "float32")

SEMAPHORES = (["q_pe", "q_act", "q_dve", "q_pool", "sent", "d_s", "d_f", "d_w", "d_l", "d_y", "sent_first"]
              + [_n + "%d" % _t for _t in range(STEPS) for _n in ("arr", "rly")]
              + ["sw%d_%d" % (_t, _k) for _t in range(STEPS) for _k in range(12)])


def routes(T, topo, r):
    me = T.cores[r]
    far = [q for q in range(N) if q != r and not topo.may_write(me, T.cores[q])]
    near = [q for q in range(N) if q != r and q not in far]
    free = sorted((c for c in topo.cores_of(me) if c != me and T.rank_of(c) is None),
                  key=lambda c: topo.die(c) != topo.die(me))
    able = [c for c in free if all(topo.may_write(c, T.cores[q]) for q in far)][:2]
    half = (len(far) + 1) // 2
    return far, near, [(able[0], far[:half]), (able[1], far[half:]), ([c for c in free if c not in able][0], near[-1:])]


def senders(T, topo, r, t):
    far, near, relays = routes(T, topo, r)
    return relays + [(T.cores[r], near[:-1])] if t >= THIRD else relays[:2] + [(T.cores[r], near)]


def deal(engines, k):
    sizes = [len(engines)]
    while len(sizes) < k:
        sizes.sort()
        big = sizes.pop()
        sizes += [big // 2, big // 2]
    sizes.sort(reverse=True)
    out, at = [], 0
    for s in sizes:
        out.append((sum(1 << e for e in engines[at:at + s]), s))
        at += s
    return out


def arrivals(T, topo, r, t):
    n = 0
    for q in range(N):
        if q != r:
            for c, ds in senders(T, topo, q, t):
                if r in ds:
                    n += deal(topo.engines(c, T.cores[r]), len(ds))[ds.index(r)][1]
    return n


def inward(T, topo, r):
    me = T.cores[r]
    far, near, relays = routes(T, topo, r)
    out = topo.engines(me, T.cores[near[0]])
    on = topo.engines(me, relays[0][0])
    return deal([e for e in on if ALL16 or e not in out], 2) + deal([e for e in on if e not in out], 1)


def given(T, t, at, n):
    return T.sb[:, t * NS + at:t * NS + at + n] if t else T.vs0[:, at:at + n]


def outward(T, topo, core, r, ds, t, at):
    tr, n = [], 0
    for i, (q, (m, k)) in enumerate(zip(ds, deal(topo.engines(core, T.cores[ds[0]]), len(ds)))):
        rid, pid = topo.addr(T.cores[q], core)
        dst = T["w%d" % t][:, A0 + r * S:A0 + (r + 1) * S] if t else T.ar0[:, r * S:(r + 1) * S]
        tr.append(RemoteDMATransfer(dst_ids=[DstId(rid=rid, pnc=pid)], dma_engine_mask=m, remote_sem=T.sem["arr%d" % t],
                                    src=given(T, t, at + i * S, S), dst=dst))
        n += k
    return tr, n


def relay_program(g, core, T, topo, r, k):
    total = 0
    for t in range(k // 2 * THIRD, STEPS):
        g.wait_ge(T.sem["rly%d" % t], inward(T, topo, r)[k][1])
        tr, n = outward(T, topo, core, r, routes(T, topo, r)[2][k][1], t, 0)
        g.remote_dma_fused(tr, local_sem=T.sem.sent)
        total += n
    if total:
        g.wait_ge(T.sem.sent, total)


def build_ops(g, core, T, topo, r):
    ops, now = [], [0]
    V, A, P = g.vector, g.scalar, g.tensor

    def op(name, alts, rd, wr, sem=None, after=()):
        ops.append({"name": (now[0], name), "alts": alts, "rd": rd, "wr": wr, "sem": sem, "after": list(after)})
        return len(ops) - 1

    def R(buf, a=0, b=1 << 20, p=0, q=128):
        return (buf, a, b, p, q)

    def ve(name, f, rd, wr):
        return op(name, {"dve": f}, rd, wr)

    def pool(name, f, rd, wr):
        return op(name, {"pool": f}, rd, wr)

    def copy(name, n, out, in_, rd, wr):
        return op(name, {"dve": lambda: V.tensor_copy(out, in_), "act": lambda: A.activation(out, in_, ACT.Copy),
                         "pool": lambda: g.affine_select(out, in_, [[0, n]], ALU.is_equal, 0.0, 0, 0)}, rd, wr)

    def mm(out, lhsT, rhs, start, stop, rd, bank):
        return op(None, {"pe": lambda: P.matmul(out, lhsT, rhs, start, stop)}, rd, [R(bank)])

    def dma(pairs, sem, rd, wr, after=(), name=None):
        q, e = ("act", A) if name else ("sp", g.sync)
        return op(name, {q: lambda: [e.dma_start(o, i) for o, i in pairs]}, rd, wr, sem=(sem, 16 * len(pairs)), after=after)

    far, near, relays = routes(T, topo, r)
    nfar = len(far) * S
    K = NS // 16

    dma([(T.s16[0:16, :], T.sends[:])], "d_s", [], [R("s16")])
    dma([(T.fl[:], T.flow[:])], "d_f", [], [R("fl")])
    dma([(T.wr[:, 1, :], T.bend[:]), (T.wr[:, 0, :], T.mix[:])], "d_w", [], [R("wr")])
    dma([(T.gi[16 * a:16 * b, :], T.links[16 * ORDER[a]:16 * (ORDER[a] + b - a), :]) for a, b in RUNS],
        "d_l", [], [R("gi")])

    imp = {"allow_small_or_imprecise_dtypes": True}
    pool("pc", lambda: g.iota(T.pc[:, 0:1], [[0, 1]], 0, 1), [], [R("pc")])
    pool("i16", lambda: g.iota(T.i16[:], [[0, K], [1, 16]], 0, 0, **imp), [], [R("i16")])
    pool("i8", lambda: g.iota(T.i8[:], [[1, 8], [0, 16]], 0, 0, **imp), [], [R("i8")])
    pool("ic", lambda: g.iota(T.ic[:], [[-16, 128]], -(W0 - H0), 0, **imp), [], [R("ic")])
    ve("ones", lambda: V.memset(T.ones[:], 1.0), [], [R("ones")])
    for a in range(2):
        o = ORDER[4 * a:4 * a + 4]
        pat = [[-16 * (o[2] - o[0]), 2], [-16 * (o[1] - o[0]), 2], [-1, 16]]
        pool("pm", lambda a=a, o=o, pat=pat: g.affine_select(T.pm[:, 64 * a:64 * a + 64], T.ones[:], pat, ALU.is_equal,
                                                             0.0, -16 * o[0], 1), [R("ones")], [R("pm", 64 * a, 64 * a + 64)])
    ve("pd0", lambda: V.tensor_scalar(T.pd[:, 0:1], T.pc[:, 0:1], 15, None, ALU.bitwise_and), [R("pc")], [R("pd", 0, 1)])
    ve("pd1", lambda: V.tensor_scalar(T.pd[:, 1:2], T.pc[:, 0:1], 4, None, ALU.arith_shift_right), [R("pc")], [R("pd", 1, 2)])
    ve("pf", lambda: V.tensor_copy(T.pf[:, 0:2], T.pd[:, 0:2]), [R("pd")], [R("pf")])
    ve("dg", lambda: V.tensor_scalar(T.dg[:], T.i16[:], T.pf[:, 0:1], None, ALU.is_equal), [R("i16"), R("pf")], [R("dg")])
    ve("nd", lambda: V.tensor_scalar(T.nd[:], T.i16[:], T.pf[:, 0:1], None, ALU.not_equal), [R("i16"), R("pf")], [R("nd")])
    ve("bo", lambda: V.tensor_scalar(T.bo[:], T.i8[:], T.pf[:, 1:2], None, ALU.is_equal), [R("i8"), R("pf")], [R("bo")])
    ve("nk", lambda: V.tensor_scalar(T.nk[:], T.ic[:], T.pf[:, 0:1], None, ALU.subtract), [R("ic"), R("pf")], [R("nk")])
    ve("mj", lambda: V.tensor_scalar(T.mj[:], T.nk[:, 0:16], float(W0 - H0 + NS), None, ALU.add), [R("nk")], [R("mj")])
    for buf, a in [("ar0", r * S)] + [("w%d" % t, A0 + r * S) for t in range(1, STEPS)]:
        copy("fill", S, T[buf][:, a:a + S], T.ones[:, 0:S], [R("ones")], [R(buf, a, a + S)])

    for k, (at, ds) in enumerate(((0, far), (len(far), near))):
        runs = []
        for i, q in enumerate(ds):
            if runs and runs[-1][1] + runs[-1][2] == q:
                runs[-1][2] += 1
            else:
                runs.append([at + i, q, 1])
        for i, q, n in runs:
            ve("sf%d" % k, lambda i=i, q=q, n=n: V.tensor_copy(T.sf[0:16, 2 * i:2 * (i + n)], T.s16[0:16, 2 * q:2 * (q + n)]),
               [R("s16")], [R("sf", 2 * i, 2 * (i + n))])
        a, b, bank = 2 * at, 2 * (at + len(ds)), "ps%d" % (6 + k)
        mm(T[bank][:, a:b], T.dg[0:16, 0:128], T.sf[0:16, a:b], True, True, [R("dg"), R("sf", a, b)], bank)
        ve("su%d" % k, lambda a=a, b=b, bank=bank: V.tensor_copy(T.su[:, a:b], T[bank][:, a:b]), [R(bank)], [R("su", a, b)])
    ve("si", lambda: V.tensor_copy(T.si[:, 0:K], T.su[:, 0:K]), [R("su")], [R("si")])
    ve("sh0", lambda: V.tensor_scalar(T.sh[:, 0:K], T.si[:, 0:K], 4, None, ALU.arith_shift_right), [R("si")], [R("sh", 0, K)])
    ve("sh1", lambda: V.tensor_scalar(T.sh[:, K:2 * K], T.si[:, 0:K], 15, None, ALU.bitwise_and), [R("si")], [R("sh", K, 2 * K)])
    ve("shu", lambda: V.tensor_copy(T.shu[:, 0:2 * K], T.sh[:, 0:2 * K]), [R("sh")], [R("shu")])

    for k, (a, b) in enumerate(RUNS):
        c = 16 * ORDER[a]
        copy("wc%d" % k, 0, T.wc[:, :, 16 * a:16 * b], T.wr[:, :, c:c + 16 * (b - a)], [R("wr")], [R("wc", 16 * a, 16 * b)])

    def rows_of_weights():
        mm(T.ps6[:, 0:128], T.pm[:], T.wc[:, 0, :], True, True, [R("pm"), R("wc")], "ps6")
        mm(T.ps6[:, 128:256], T.pm[:], T.wc[:, 1, :], True, True, [R("pm"), R("wc")], "ps6")
        copy("wf", 256, T.wf[:], T.ps6[:, 0:256], [R("ps6")], [R("wf")])
        copy("wb", 256, T.wb[:], T.wf[:], [R("wf")], [R("wb")])

    def offsets():
        now[0] = 1
        ve("gt", lambda: V.tensor_tensor(T.gt[:], T.gi[:], T.nk[:], ALU.mult), [R("gi"), R("nk")], [R("gt")])
        ve("go", lambda: V.tensor_tensor(T.go[:], T.gi[:], T.gt[:], ALU.max), [R("gi"), R("gt")], [R("go")])
        ve("off", lambda: V.tensor_copy(T.off[:], T.go[:]), [R("go")], [R("off")])
        now[0] = 0
        copy("m1", NS, T.m1[:], T.dg[:, 0:16].indirect(T.shu[:, K:2 * K]), [R("dg"), R("shu")], [R("m1")])
        ve("qm", lambda: V.tensor_tensor(T.qm[:], T.gi[:, 0:128].indirect(T.shu[:, 0:K]), T.m1[:], ALU.mult),
           [R("gi"), R("shu"), R("m1")], [R("qm")])
        mm(T.ps7[:, 0:NS], T.bo[:], T.qm[:], True, True, [R("bo"), R("qm")], "ps7")
        ve("rd", lambda: V.tensor_tensor(T.rd[:], T.ps7[:, 0:NS], T.dg[:], ALU.mult), [R("ps7"), R("dg")], [R("rd")])
        ve("sc", lambda: V.tensor_tensor_scan(T.sc[:], T.nd[:], T.rd[:], 0.0, ALU.mult, ALU.add), [R("nd"), R("rd")], [R("sc")])
        ve("t1", lambda: V.tensor_tensor(T.t1[:, 0:K], T.sc[:, 15:NS:16], T.mj[:, 0:K], ALU.mult), [R("sc"), R("mj")], [R("t1")])
        ve("t2", lambda: V.tensor_tensor(T.t2[:, 0:K], T.sc[:, 15:NS:16], T.t1[:, 0:K], ALU.min), [R("sc"), R("t1")], [R("t2")])
        ve("offs", lambda: V.tensor_scalar(T.offs[:, 0:K], T.t2[:, 0:K], float(NS), None, ALU.add), [R("t2")], [R("offs")])

    turn = [0]
    root = math.sqrt(0.125)

    def collide(k, n, pieces, wbuf, x, out, outr, swapped=False):
        ba, bb = "ps%d" % (turn[0] % BANKS), "ps%d" % (turn[0] % BANKS + 1)
        turn[0] += 2
        for j, bank in ((1, bb), (0, ba)):
            for i, (ap, reg) in enumerate(pieces):
                for p, q, z in ((0, 64, 64), (64, 128, 0)) if swapped else ((0, 128, 0),):
                    w = T.wc[:, j, z:z + q - p] if wbuf == "wc" else T[wbuf][:, 128 * j:128 * j + 128]
                    mm(T[bank][p:q, 0:n], w, ap, i == 0, i == len(pieces) - 1, [R(wbuf), reg], bank)
        op("s" + k, {"act": lambda: A.activation(T.sq[:, x:x + n], T[bb][:, 0:n], ACT.Square, scale=root)},
           [R(bb)], [R("sq", x, x + n)])
        ve("a" + k, lambda: V.tensor_tensor(out, T[ba][:, 0:n], T.sq[:, x:x + n], ALU.add), [R(ba), R("sq", x, x + n)], [outr])

    def swap(sname, a, n, wn, b, sem, k=None, after=()):
        src = T[sname]
        if k is None:
            dma([(T[wn][64:128, b:b + n], src[0:64, a:a + n]), (T[wn][0:64, b:b + n], src[64:128, a:a + n])],
                sem, [R(sname, a, a + n)], [R(wn, b, b + n)], after)
        else:
            for name, p in (("d", 0), ("u", 64)):
                copy(name + k, n, T[wn][64 - p:128 - p, b:b + n], src[p:p + 64, a:a + n], [R(sname, a, a + n)],
                     [R(wn, b, b + n, 64 - p, 128 - p)])

    def call(t, part):
        tr, n = outward(T, topo, core, r, senders(T, topo, r, t)[-1][1], t, nfar) if part else ([], 0)
        for (c, ds), (m, k) in list(zip(relays, inward(T, topo, r)))[2 * part:2 + (t >= THIRD) * part]:
            rid, pid = topo.addr(c, core)
            at, wd = (far + near).index(ds[0]) * S, len(ds) * S
            tr.append(RemoteDMATransfer(dst_ids=[DstId(rid=rid, pnc=pid)], dma_engine_mask=m,
                                        remote_sem=T.sem["rly%d" % t], src=given(T, t, at, wd), dst=given(T, t, 0, wd)))
            n += k
        a, b = (0, nfar) if part == 0 else (nfar, NS)
        sem = "sent" if t + part else "sent_first"
        return op(("far", "near")[part], {"pool": lambda: g.remote_dma_fused(tr, local_sem=T.sem[sem])},
                  [R("sb", t * NS + a, t * NS + b) if t else R("vs0", a, b)], [], sem=(sem, n))

    for t in range(STEPS):
        now[0] = t
        wn, wp = "w%d" % t, "w%d" % (t - 1)
        listed = " ".join(QUEUES[t].values()).split()
        calls, b = [], 0
        for k, n in zip("ABC", GIVEN):
            a, b = b, b + n
            x = t * NS + a
            if t == 0:
                copy("g" + k, n, T.vs0[:, a:b], T.fl[:, 0:C].indirect(T.su[:, a // 16:b // 16]), [R("fl"), R("su", a // 16, b // 16)],
                     [R("vs0", a, b)])
            else:
                copy("g" + k, n, T.vf[:, a:b], T[wp][:, 0:A0].indirect(T.offs[:, a // 16:b // 16]),
                     [R(wp, 0, A0), R("offs")], [R("vf", a, b)])
                collide(k, n, [(T.vf[:, a:b], R("vf", a, b))], "wf", a, T.sb[:, x:x + n], R("sb", x, x + n))
            calls += [call(t, part) for part, e in enumerate((nfar, NS)) if e == b]
        if 0 < t < STEPS - 1:
            swap("sb", t * NS, NS, wn, 0, "sw%d_11" % t)
        blocks = [R(wn, A0 + q * S, A0 + (q + 1) * S) if t else R("ar0", q * S, (q + 1) * S) for q in range(N) if q != r]
        op(None, {None: None}, [], blocks, sem=("arr%d" % t, arrivals(T, topo, r, t)))
        if t == 1:
            b = 0
            for k, n in zip("XY", TAKEN):
                a, b = b, b + n
                collide(k, n, [(T.ar0[:, a:b], R("ar0", a, b))], "wc", NS + C + a, T[wp][:, A0 + a:A0 + b],
                        R(wp, A0 + a, A0 + b))
        c0 = s0 = 0
        chunks = (FIRST, SECOND, MAIN)[min(t, 2)].split()
        for j, spec in enumerate(chunks):
            k, n, mode = str(j), int(spec[:-1]), spec[-1]
            c1, x = c0 + n, NS + c0
            out, outr = T[wn][:, H0 + c0:H0 + c1], R(wn, H0 + c0, H0 + c1)
            if mode != "b":
                src = T[wp][:, H0:W0 + c1].indirect(T.off[:, c0 // 16:c1 // 16])
                rd = [R(wp, H0, W0 + c1), R("off")]
            if mode == "b":
                collide(k, n, [(T.fl[:, c0:c1], R("fl"))], "wc", x, out, outr)
            elif mode == "f":
                copy("g" + k, n, T.vf[:, x:x + n], src, rd, [R("vf", x, x + n)])
                collide(k, n, [(T.vf[:, x:x + n], R("vf", x, x + n))], "wf", x, out, outr)
                if c1 == C:
                    ops[-4]["early"] = 3 if chunks[-2][-1] == "s" else 1
            else:
                hi, md, lo, rr = T.hi[:, c0:c1], T.md[:, c0:c1], T.lo[:, c0:c1], T.rr[:, c0:c1]
                copy("g" + k, n, hi, src, rd, [R("hi", c0, c1)])
                ve("r" + k, lambda rr=rr, src=src, hi=hi: V.tensor_tensor(rr, src, hi, ALU.subtract),
                   rd + [R("hi", c0, c1)], [R("rr", c0, c1)])
                copy("m" + k, n, md, rr, [R("rr", c0, c1)], [R("md", c0, c1)])
                rp, reg = rr, R("rr", c0, c1)
                if "p" + k in listed:
                    bank = "ps%d" % (6 + j % 2)
                    rp, reg = T[bank][:, 0:n], R(bank)
                    copy("p" + k, n, rp, rr, [R("rr", c0, c1)], [reg])
                ve("l" + k, lambda lo=lo, rp=rp, md=md: V.tensor_tensor(lo, rp, md, ALU.subtract),
                   [reg, R("md", c0, c1)], [R("lo", c0, c1)])
                collide(k, n, [(hi, R("hi", c0, c1)), (md, R("md", c0, c1)), (lo, R("lo", c0, c1))], "wb", x, out, outr)
            if "u" + k in listed:
                swap(wn, H0 + c0, n, wn, W0 + c0, None, k)
                s0 = c1
            elif c1 - s0 >= MERGE or c1 == C or "u%d" % (j + 1) in listed:
                swap(wn, H0 + s0, c1 - s0, wn, W0 + s0, "sw%d_%d" % (t, j), None, calls[:1] if t == 0 else ())
                s0 = c1
            c0 = c1
            if t == 0 and j in (1, 2):
                (rows_of_weights, offsets)[j - 1]()
        if t == 0:
            collide("Z", NS, [(T.vs0[:], R("vs0"))], "wc", 0, T[wn][:, 0:NS], R(wn, 0, NS), swapped=True)

    wp = "w%d" % (STEPS - 1)
    b = 0
    for k, n in enumerate(LAST):
        a, b = b, b + n
        copy("y%d" % k, n, T.vf[:, NS + a:NS + b], T[wp][:, H0:W0 + b].indirect(T.off[:, a // 16:b // 16]),
             [R(wp, H0, W0 + b), R("off")], [R("vf", NS + a, NS + b)])
        if k % 2:
            a -= LAST[k - 1]
            pairs = [(T.y[16 * ORDER[i]:16 * (ORDER[i] + j - i), a:b], T.vf[16 * i:16 * j, NS + a:NS + b]) for i, j in RUNS]
            cut = 3 if "o%d" % k in listed else len(RUNS)
            dma(pairs[:cut], "d_y", [R("vf", NS + a, NS + b)], [])
            if pairs[cut:]:
                dma(pairs[cut:], "d_y", [R("vf", NS + a, NS + b)], [], name="o%d" % k)
    return ops


def order_ops(ops):
    seen = {}
    for i, o in enumerate(ops):
        dep = set(o["after"])
        acc = [(x, x[0].startswith("ps")) for x in o["rd"]] + [(x, True) for x in o["wr"]]
        for x, w in acc:
            for j, y, v in seen.get(x[0], []):
                if (w or v) and x[1] < y[2] and y[1] < x[2] and x[3] < y[4] and y[3] < x[4]:
                    dep.add(j)
        for x, w in acc:
            lst = seen.setdefault(x[0], [])
            if w:
                lst[:] = [e for e in lst if not (x[1] <= e[1][1] and e[1][2] <= x[2] and x[3] <= e[1][3] and e[1][4] <= x[4])]
            lst.append((i, x, w))
        o["dep"] = dep
    lines = {}
    for i, o in enumerate(ops):
        if o["name"][1] is None:
            line = lines.setdefault(list(o["alts"])[0], [])
            line.insert(len(line) - o.get("early", 0), i)
    for t, queues in enumerate(QUEUES):
        for q, names in queues.items():
            for name in names.split():
                lines.setdefault(q, []).extend(i for i, o in enumerate(ops) if o["name"] == (t, name))
    seq, done = [], set()
    while len(seq) < len(ops):
        q = [q for q, line in lines.items() if line and ops[line[0]]["dep"] <= done][0]
        i = lines[q].pop(0)
        ops[i]["q"] = q
        seq.append(i)
        done.add(i)
    return seq


def rank_program(g, core, T, topo):
    r = T.rank_of(core)
    if r is None:
        for q in range(N):
            for k, (c, ds) in enumerate(routes(T, topo, q)[2]):
                if c == core:
                    relay_program(g, core, T, topo, q, k)
        return
    ops = build_ops(g, core, T, topo, r)
    eng = {"pe": g.tensor, "act": g.scalar, "dve": g.vector, "pool": g, "sp": g.sync}
    known = {q: {} for q in eng}
    total = {}
    for i in order_ops(ops):
        o = ops[i]
        q = o["q"]
        if q is None:
            o["mark"], o["clock"] = o["sem"], {o["sem"][0]: o["sem"][1]}
            total[o["sem"][0]] = o["sem"][1]
            continue
        kn = known[q]
        for j in sorted(o["dep"], reverse=True):
            d = ops[j]
            s, v = d["mark"]
            if (q == "pe" and d["q"] == "pe") or kn.get(s, 0) >= v:
                continue
            eng[q].wait_ge(T.sem[s], v)
            for s2, v2 in d["clock"].items():
                kn[s2] = max(kn.get(s2, 0), v2)
        res = o["alts"][q]()
        s, v = o["sem"] or ("q_" + q, 1)
        total[s] = total.get(s, 0) + v
        if o["sem"] is None:
            res.then_inc(T.sem[s], 1)
        elif q != "pool":
            for ins in res:
                ins.then_inc(T.sem[s], 16)
        o["mark"] = (s, total[s])
        o["clock"] = dict(kn)
        o["clock"][s] = total[s]
    for s, v in total.items():
        if max(known[q].get(s, 0) for q in known) < v:
            (g.sync if s == "d_y" else g).wait_ge(T.sem[s], v)
